import numpy as np
import ml_dtypes


def mxq(x, axis, fmt="e4m3"):
    dtype, down = {"e4m3": (ml_dtypes.float8_e4m3fn, 7), "e5m2": (ml_dtypes.float8_e5m2, 14)}[fmt]
    v = np.moveaxis(np.asarray(x, np.float32).astype(ml_dtypes.bfloat16).astype(np.float64), axis, -1)
    blocks = v.reshape(v.shape[:-1] + (-1, 32))
    amax = np.abs(blocks).max(-1, keepdims=True)
    byte = np.maximum(np.where(amax > 0, np.frexp(amax)[1] - 1 + 127, 0) - down, 1)
    scale = np.exp2(byte - 127.0)
    codes = (blocks / scale).astype(np.float32).astype(dtype).astype(np.float64)
    return np.moveaxis((codes * scale).reshape(v.shape), -1, axis)


WIDE = False


def mx_kscale(k):
    if not WIDE:
        return np.ones(k)
    levels = np.array([10, -10, 5, -5, 0])
    if k % 512:
        return np.exp2(np.random.permutation(np.resize(levels, k // 32))).repeat(32)
    a = np.empty((k // 512, 16))
    for p in range(k // 512):
        a[p, :8] = np.random.permutation(np.resize(levels, 8))
        for g in range(8):
            far = levels[np.abs(levels - a[p, g]) >= 10]
            a[p, g + 8] = far[np.random.randint(len(far))]
    return np.exp2(a.ravel()).repeat(32)


def f64(x):
    return np.asarray(x).astype(np.float64)


def striped(idx):
    return np.tile(idx.reshape(-1, 16).T, (8, 1)).astype(np.uint16)


def unstriped(offs):
    return offs[:16].T.reshape(-1).astype(np.int64)


def pack_weight(w):
    k, n = w.shape
    w = f64(np.asarray(w, np.float32).astype(ml_dtypes.bfloat16)).reshape(k // 32, 32, n)
    amax = np.abs(w).max(1)
    byte = np.clip(np.where(amax > 0, np.frexp(amax)[1] - 1 + 127 - 7, 1), 1, 254)
    scaled = (w * np.exp2(127.0 - byte)[:, None, :]).reshape(k, n).astype(np.float32)
    words = np.ascontiguousarray(scaled.reshape(k // 512, 128, 4, n).transpose(0, 1, 3, 2)).astype(ml_dtypes.float8_e4m3fn).view(np.uint8)
    return words, np.ascontiguousarray(byte.astype(np.uint8).reshape(k // 512, 16, n))


def unpack_weight(words, scales):
    g, p, n, _ = words.shape
    vals = np.ascontiguousarray(words).view(ml_dtypes.float8_e4m3fn).astype(np.float64) * np.repeat(np.exp2(scales.astype(np.float64) - 127.0), 8, axis=1)[..., None]
    return vals.transpose(0, 1, 3, 2).reshape(g * 512, n)


def gelu(v):
    return 0.5 * v * (1.0 + np.tanh(np.sqrt(2.0 / np.pi) * (v + 0.044715 * v**3)))


K, T, S, H, N = 1024, 1024, 512, 512, 256


def setup_inputs():
    n = np.random.standard_normal
    s = mx_kscale(K)[:, None]
    u = mx_kscale(H)
    packed_xT = pack_weight(n((K, T)) * s)
    return {
        "x_words": packed_xT[0],
        "x_scales": packed_xT[1],
        "w1": (n((K, H)) / np.sqrt(K) / s * u).astype(np.float32),
        "w2": (n((H, N)) / np.sqrt(H) / u[:, None]).astype(np.float32),
        "pe": (0.5 * n((H, T)) * u[:, None]).astype(np.float32),
        "offs": striped(np.random.permutation(T)[:S]),
    }


def reference(x_words, x_scales, w1, w2, pe, offs):
    xq = unpack_weight(x_words, x_scales)[:, unstriped(offs)]
    g = f64(pe)[:, unstriped(offs)]
    h = gelu((mxq(f64(w1), 0, "e4m3").T @ xq) + g)
    return mxq(f64(w2), 0, "e4m3").T @ mxq(h, 0, "e4m3")

@@ -1,0 +1,181 @@
+from contextlib import ExitStack
+
+import concourse.mybir as mybir
+
+K, T, S, H, N = 1024, 1024, 512, 512, 256
+FLOPS = 2 * K * H * S + 2 * H * N * S
+
+F32 = mybir.dt.float32
+BF16 = mybir.dt.bfloat16
+I32 = mybir.dt.int32
+U32 = mybir.dt.uint32
+U16 = mybir.dt.uint16
+U8 = mybir.dt.uint8
+FP8X4 = mybir.dt.float8_e4m3fn_x4
+GELU = mybir.ActivationFunctionType.Gelu_apprx_tanh
+ADD = mybir.AluOpType.add
+
+P = 128
+PACK = 4
+PASSES = K // (P * PACK)
+HALF = S // 2
+VECTOR_M = 80
+CHUNKS = [(0, 256), (256, 128), (384, 128)]
+
+
+def tile_picked_posadd_gelu_p_kernel(tc, x_words, x_scales, w1, w2, pe, offs, out):
+    nc = tc.nc
+    with ExitStack() as ctx:
+        sb = ctx.enter_context(tc.tile_pool(name="sb", bufs=1))
+        ps = ctx.enter_context(tc.psum_pool(name="ps", bufs=1))
+
+        offsets = sb.tile([P, S // 16], U16, name="offsets")
+        nc.sync.dma_start(offsets[:], offs)
+
+        def picks(first, count):
+            return offsets[:, first // 16 : (first + count) // 16]
+
+        scale_table = sb.tile([P, T], U8, name="scale_table", align_bytes=64)
+        nc.vector.memset(scale_table[:].bitcast(I32), 0)
+        zero = sb.tile([P, 1], F32, name="zero")
+        nc.vector.memset(zero[:], 0.0)
+        zero_bias = sb.tile([P, 1], F32, name="zero_bias")
+        nc.scalar.activation(zero_bias[:], zero[:], GELU)
+
+        word_table = [sb.tile([P, T], I32, name=f"word_table{z}", align_bytes=64) for z in range(PASSES)]
+        w1_raw = [sb.tile([P, PACK, H], F32, name=f"w1_raw{z}", align_bytes=64) for z in range(PASSES)]
+        pe_table = [sb.tile([P, T], F32, name=f"pe_table{t}", align_bytes=64) for t in range(PACK)]
+        w2_raw = sb.tile([P, PACK, N], F32, name="w2_raw", align_bytes=64)
+
+        def load_words(z):
+            nc.sync.dma_start(word_table[z][:], x_words[z].rearrange("p c r -> p (c r)").bitcast(I32))
+
+        def load_w1(z):
+            nc.sync.dma_start(w1_raw[z][:], w1[z * 512 : (z + 1) * 512, :].rearrange("(p j) c -> p j c", j=PACK))
+
+        load_words(0)
+        for q in range(4):
+            nc.sync.dma_start(
+                scale_table[32 * q : 32 * q + 8, :].bitcast(I32),
+                x_scales[:, 4 * q : 4 * q + 4, :].bitcast(I32),
+            )
+        load_w1(0)
+        load_words(1)
+        load_w1(1)
+        pe_rows = pe.rearrange("(p t) c -> t p c", t=PACK)
+        for t in range(PACK):
+            nc.sync.dma_start(pe_table[t][:], pe_rows[t])
+            if t == 1:
+                nc.sync.dma_start(w2_raw[:], w2.rearrange("(p j) m -> p j m", j=PACK))
+
+        x_codes = [sb.tile([P, S], U32, name=f"x_codes{z}", align_bytes=64) for z in range(PASSES)]
+        x_bytes = sb.tile([P, S], U8, name="x_bytes", align_bytes=64)
+        w1_bf = [sb.tile([P, PACK, P, PACK], BF16, name=f"w1_bf{z}", align_bytes=64) for z in range(PASSES)]
+        w1_codes = [sb.tile([P, H], U32, name=f"w1_codes{z}", align_bytes=64) for z in range(PASSES)]
+        w1_bytes = [sb.tile([P, H], U8, name=f"w1_bytes{z}", align_bytes=64) for z in range(PASSES)]
+
+        def gather_words(z):
+            nc.vector.tensor_copy(x_codes[z][:], word_table[z][:].bitcast(U32).indirect(offsets[:]))
+
+        def quantize_w1(z):
+            src = w1_raw[z][:].rearrange("p j (m t) -> p m t j", t=PACK)
+            dst = w1_bf[z][:].rearrange("p t m j -> p m t j")
+            nc.vector.tensor_copy(dst[:, :VECTOR_M], src[:, :VECTOR_M])
+            nc.scalar.copy(dst[:, VECTOR_M:], src[:, VECTOR_M:])
+            nc.vector.quantize_mx(
+                out=w1_codes[z][:].bitcast(FP8X4),
+                scales=w1_bytes[z][:],
+                in_=w1_bf[z][:].rearrange("p t m j -> p (t m j)"),
+            )
+
+        gather_words(0)
+        nc.vector.tensor_copy(x_bytes[:], scale_table[:].indirect(offsets[:]))
+        quantize_w1(0)
+        gather_words(1)
+        quantize_w1(1)
+
+        acc = {}
+        for pair in range(2):
+            for half in range(2):
+                acc[pair, half] = ps.tile([P, 2, HALF], F32, name=f"acc{pair}{half}")
+                cols = slice(half * HALF, (half + 1) * HALF)
+                for e in range(2):
+                    t = 2 * pair + e
+                    for z in range(PASSES):
+                        nc.tensor.matmul_mx(
+                            out=acc[pair, half][:, e, :],
+                            lhsT=w1_codes[z][:, t * P : (t + 1) * P].bitcast(FP8X4),
+                            lhsT_scale=w1_bytes[z][:, t * P : (t + 1) * P],
+                            rhs=x_codes[z][:, cols].bitcast(FP8X4),
+                            rhs_scale=x_bytes[4 * z : P, cols],
+                            start=(z == 0),
+                            stop=(z == PASSES - 1),
+                        )
+
+        pe_picked = [sb.tile([P, 2, S], F32, name=f"pe_picked{pair}", align_bytes=64) for pair in range(2)]
+        pre = [sb.tile([P, 2, S], F32, name=f"pre{pair}", align_bytes=64) for pair in range(2)]
+        h_bf = sb.tile([P, S, PACK], BF16, name="h_bf", align_bytes=64)
+
+        def gather_pe(t, first, count):
+            nc.vector.tensor_copy(
+                pe_picked[t // 2][:, t % 2, first : first + count], pe_table[t][:].indirect(picks(first, count))
+            )
+
+        def add_and_gelu(pair, first, count):
+            half, inner = divmod(first, HALF)
+            cols = slice(first, first + count)
+            nc.vector.tensor_tensor(
+                pre[pair][:, :, cols], acc[pair, half][:, :, inner : inner + count], pe_picked[pair][:, :, cols], ADD
+            )
+            nc.scalar.activation(
+                h_bf[:, cols, 2 * pair : 2 * pair + 2],
+                pre[pair][:, :, cols].rearrange("p e j -> p j e"),
+                GELU,
+                bias=zero_bias[:],
+            )
+
+        gather_pe(0, 0, S)
+        gather_pe(1, 0, S)
+        w2_bf = sb.tile([P, N, PACK], BF16, name="w2_bf", align_bytes=64)
+        nc.scalar.copy(w2_bf[:], w2_raw[:].rearrange("p j m -> p m j"))
+        add_and_gelu(0, 0, HALF)
+        add_and_gelu(0, HALF, HALF)
+        gather_pe(2, 0, S)
+
+        w2_codes = sb.tile([P, N], U32, name="w2_codes", align_bytes=64)
+        w2_bytes = sb.tile([P, N], U8, name="w2_bytes", align_bytes=64)
+        h_codes = sb.tile([P, S], U32, name="h_codes", align_bytes=64)
+        h_bytes = sb.tile([P, S], U8, name="h_bytes", align_bytes=64)
+        out_rows = out.rearrange("(b p) s -> p b s", p=P)
+        nc.vector.quantize_mx(
+            out=w2_codes[:].bitcast(FP8X4), scales=w2_bytes[:], in_=w2_bf[:].rearrange("p m j -> p (m j)")
+        )
+
+        for first, count in CHUNKS:
+            gather_pe(3, first, count)
+            add_and_gelu(1, first, count)
+
+        for first, count in CHUNKS:
+            cols = slice(first, first + count)
+            nc.vector.quantize_mx(
+                out=h_codes[:, cols].bitcast(FP8X4),
+                scales=h_bytes[:, cols],
+                in_=h_bf[:, cols, :].rearrange("p j t -> p (j t)"),
+            )
+            res = ps.tile([P, 2, count], F32, name=f"res{first}")
+            for b in range(N // P):
+                nc.tensor.matmul_mx(
+                    out=res[:, b, :],
+                    lhsT=w2_codes[:, b * P : (b + 1) * P].bitcast(FP8X4),
+                    lhsT_scale=w2_bytes[:, b * P : (b + 1) * P],
+                    rhs=h_codes[:, cols].bitcast(FP8X4),
+                    rhs_scale=h_bytes[:, cols],
+                    start=True,
+                    stop=True,
+                )
+            staged = sb.tile([P, 2, count], F32, name=f"staged{first}")
+            if first == 0:
+                nc.scalar.copy(staged[:], res[:])
+            else:
+                nc.vector.tensor_copy(staged[:], res[:])
+            nc.sync.dma_start(out_rows[:, :, cols], staged[:])

@@ -19,7 +19,7 @@ P = 128
 PACK = 4
 PASSES = K // (P * PACK)
 HALF = S // 2
-VECTOR_M = 80
+VECTOR_M = [32, 80]
 CHUNKS = [(0, 256), (256, 128), (384, 128)]
 
 
@@ -80,8 +80,8 @@ def tile_picked_posadd_gelu_p_kernel(tc, x_words, x_scales, w1, w2, pe, offs, ou
         def quantize_w1(z):
             src = w1_raw[z][:].rearrange("p j (m t) -> p m t j", t=PACK)
             dst = w1_bf[z][:].rearrange("p t m j -> p m t j")
-            nc.vector.tensor_copy(dst[:, :VECTOR_M], src[:, :VECTOR_M])
-            nc.scalar.copy(dst[:, VECTOR_M:], src[:, VECTOR_M:])
+            nc.vector.tensor_copy(dst[:, : VECTOR_M[z]], src[:, : VECTOR_M[z]])
+            nc.scalar.copy(dst[:, VECTOR_M[z] :], src[:, VECTOR_M[z] :])
             nc.vector.quantize_mx(
                 out=w1_codes[z][:].bitcast(FP8X4),
                 scales=w1_bytes[z][:],
@@ -112,27 +112,40 @@ def tile_picked_posadd_gelu_p_kernel(tc, x_words, x_scales, w1, w2, pe, offs, ou
                             stop=(z == PASSES - 1),
                         )
 
-        pe_picked = [sb.tile([P, 2, S], F32, name=f"pe_picked{pair}", align_bytes=64) for pair in range(2)]
-        pre = [sb.tile([P, 2, S], F32, name=f"pre{pair}", align_bytes=64) for pair in range(2)]
-        h_bf = sb.tile([P, S, PACK], BF16, name="h_bf", align_bytes=64)
+        early = sb.tile([P, 2, S], F32, name="early", align_bytes=64)
+        late = sb.tile([P, 2 * S], F32, name="late", align_bytes=64)
+
+        def picked(pair, first, count):
+            if pair == 0:
+                return early[:, :, first : first + count]
+            if first < HALF:
+                return late[:].rearrange("p (e j) -> p e j", e=2)[:, :, first : first + count]
+            return late[:, HALF : 3 * HALF].rearrange("p (e j) -> p e j", e=2)[:, :, first - HALF : first - HALF + count]
+
+        h_bf = {first: sb.tile([P, count, PACK], BF16, name=f"h_bf{first}", align_bytes=64) for first, count in CHUNKS}
 
         def gather_pe(t, first, count):
-            nc.vector.tensor_copy(
-                pe_picked[t // 2][:, t % 2, first : first + count], pe_table[t][:].indirect(picks(first, count))
-            )
+            dst = late[:, 0:S] if t == 2 else picked(t // 2, first, count)[:, t % 2, :]
+            nc.vector.tensor_copy(dst, pe_table[t][:].indirect(picks(first, count)))
 
         def add_and_gelu(pair, first, count):
             half, inner = divmod(first, HALF)
-            cols = slice(first, first + count)
+            pre = sb.tile([P, 2, count], F32, name=f"pre{pair}_{first}", align_bytes=64)
             nc.vector.tensor_tensor(
-                pre[pair][:, :, cols], acc[pair, half][:, :, inner : inner + count], pe_picked[pair][:, :, cols], ADD
+                pre[:], acc[pair, half][:, :, inner : inner + count], picked(pair, first, count), ADD
             )
-            nc.scalar.activation(
-                h_bf[:, cols, 2 * pair : 2 * pair + 2],
-                pre[pair][:, :, cols].rearrange("p e j -> p j e"),
-                GELU,
-                bias=zero_bias[:],
-            )
+            gelu(pair, pre, first, count)
+
+        def gelu(pair, pre, first, count):
+            for start, width in CHUNKS:
+                lo, hi = max(first, start), min(first + count, start + width)
+                if lo < hi:
+                    nc.scalar.activation(
+                        h_bf[start][:, lo - start : hi - start, 2 * pair : 2 * pair + 2],
+                        pre[:, :, lo - first : hi - first].rearrange("p e j -> p j e"),
+                        GELU,
+                        bias=zero_bias[:],
+                    )
 
         gather_pe(0, 0, S)
         gather_pe(1, 0, S)
@@ -144,38 +157,45 @@ def tile_picked_posadd_gelu_p_kernel(tc, x_words, x_scales, w1, w2, pe, offs, ou
 
         w2_codes = sb.tile([P, N], U32, name="w2_codes", align_bytes=64)
         w2_bytes = sb.tile([P, N], U8, name="w2_bytes", align_bytes=64)
-        h_codes = sb.tile([P, S], U32, name="h_codes", align_bytes=64)
-        h_bytes = sb.tile([P, S], U8, name="h_bytes", align_bytes=64)
         out_rows = out.rearrange("(b p) s -> p b s", p=P)
         nc.vector.quantize_mx(
             out=w2_codes[:].bitcast(FP8X4), scales=w2_bytes[:], in_=w2_bf[:].rearrange("p m j -> p (m j)")
         )
 
-        for first, count in CHUNKS:
-            gather_pe(3, first, count)
-            add_and_gelu(1, first, count)
+        for half in range(2):
+            for quarter in range(2):
+                gather_pe(3, half * HALF + quarter * 128, 128)
+            for quarter in range(2):
+                add_and_gelu(1, half * HALF + quarter * 128, 128)
 
         for first, count in CHUNKS:
             cols = slice(first, first + count)
+            h_codes = sb.tile([P, count], U32, name=f"h_codes{first}", align_bytes=64)
+            h_bytes = sb.tile([P, count], U8, name=f"h_bytes{first}", align_bytes=64)
             nc.vector.quantize_mx(
-                out=h_codes[:, cols].bitcast(FP8X4),
-                scales=h_bytes[:, cols],
-                in_=h_bf[:, cols, :].rearrange("p j t -> p (j t)"),
+                out=h_codes[:].bitcast(FP8X4), scales=h_bytes[:], in_=h_bf[first][:].rearrange("p j t -> p (j t)")
             )
-            res = ps.tile([P, 2, count], F32, name=f"res{first}")
+            if first == 0:
+                res = [ps.tile([P, count], F32, name=f"res{first}_{b}")[:] for b in range(2)]
+            else:
+                both = ps.tile([P, 2, count], F32, name=f"res{first}")
+                res = [both[:, b, :] for b in range(2)]
             for b in range(N // P):
                 nc.tensor.matmul_mx(
-                    out=res[:, b, :],
+                    out=res[b],
                     lhsT=w2_codes[:, b * P : (b + 1) * P].bitcast(FP8X4),
                     lhsT_scale=w2_bytes[:, b * P : (b + 1) * P],
-                    rhs=h_codes[:, cols].bitcast(FP8X4),
-                    rhs_scale=h_bytes[:, cols],
+                    rhs=h_codes[:].bitcast(FP8X4),
+                    rhs_scale=h_bytes[:],
                     start=True,
                     stop=True,
                 )
-            staged = sb.tile([P, 2, count], F32, name=f"staged{first}")
             if first == 0:
-                nc.scalar.copy(staged[:], res[:])
+                for b in range(2):
+                    staged = sb.tile([P, count], F32, name=f"staged{first}_{b}")
+                    nc.scalar.copy(staged[:], res[b])
+                    nc.sync.dma_start(out_rows[:, b, cols], staged[:])
             else:
-                nc.vector.tensor_copy(staged[:], res[:])
-            nc.sync.dma_start(out_rows[:, :, cols], staged[:])
+                staged = sb.tile([P, 2, count], F32, name=f"staged{first}")
+                nc.vector.tensor_copy(staged[:], both[:])
+                nc.sync.dma_start(out_rows[:, :, cols], staged[:])

@@ -19,7 +19,7 @@ P = 128
 PACK = 4
 PASSES = K // (P * PACK)
 HALF = S // 2
-VECTOR_M = [32, 80]
+VECTOR_M = [80, 80]
 CHUNKS = [(0, 256), (256, 128), (384, 128)]
 
 
@@ -45,7 +45,7 @@ def tile_picked_posadd_gelu_p_kernel(tc, x_words, x_scales, w1, w2, pe, offs, ou
         word_table = [sb.tile([P, T], I32, name=f"word_table{z}", align_bytes=64) for z in range(PASSES)]
         w1_raw = [sb.tile([P, PACK, H], F32, name=f"w1_raw{z}", align_bytes=64) for z in range(PASSES)]
         pe_table = [sb.tile([P, T], F32, name=f"pe_table{t}", align_bytes=64) for t in range(PACK)]
-        w2_raw = sb.tile([P, PACK, N], F32, name="w2_raw", align_bytes=64)
+        w2_raw = sb.tile([P, PACK, N], F32, name="w2_raw", tag="w2_then_h", align_bytes=64)
 
         def load_words(z):
             nc.sync.dma_start(word_table[z][:], x_words[z].rearrange("p c r -> p (c r)").bitcast(I32))
@@ -54,13 +54,13 @@ def tile_picked_posadd_gelu_p_kernel(tc, x_words, x_scales, w1, w2, pe, offs, ou
             nc.sync.dma_start(w1_raw[z][:], w1[z * 512 : (z + 1) * 512, :].rearrange("(p j) c -> p j c", j=PACK))
 
         load_words(0)
+        load_words(1)
         for q in range(4):
             nc.sync.dma_start(
                 scale_table[32 * q : 32 * q + 8, :].bitcast(I32),
                 x_scales[:, 4 * q : 4 * q + 4, :].bitcast(I32),
             )
         load_w1(0)
-        load_words(1)
         load_w1(1)
         pe_rows = pe.rearrange("(p t) c -> t p c", t=PACK)
         for t in range(PACK):
@@ -89,9 +89,9 @@ def tile_picked_posadd_gelu_p_kernel(tc, x_words, x_scales, w1, w2, pe, offs, ou
             )
 
         gather_words(0)
+        gather_words(1)
         nc.vector.tensor_copy(x_bytes[:], scale_table[:].indirect(offsets[:]))
         quantize_w1(0)
-        gather_words(1)
         quantize_w1(1)
 
         acc = {}
@@ -122,7 +122,8 @@ def tile_picked_posadd_gelu_p_kernel(tc, x_words, x_scales, w1, w2, pe, offs, ou
                 return late[:].rearrange("p (e j) -> p e j", e=2)[:, :, first : first + count]
             return late[:, HALF : 3 * HALF].rearrange("p (e j) -> p e j", e=2)[:, :, first - HALF : first - HALF + count]
 
-        h_bf = {first: sb.tile([P, count, PACK], BF16, name=f"h_bf{first}", align_bytes=64) for first, count in CHUNKS}
+        h_all = sb.tile([P, S, PACK], BF16, name="h_all", tag="w2_then_h", align_bytes=64)
+        h_bf = {first: h_all[:, first : first + count, :] for first, count in CHUNKS}
 
         def gather_pe(t, first, count):
             dst = late[:, 0:S] if t == 2 else picked(t // 2, first, count)[:, t % 2, :]
@@ -173,7 +174,7 @@ def tile_picked_posadd_gelu_p_kernel(tc, x_words, x_scales, w1, w2, pe, offs, ou
             h_codes = sb.tile([P, count], U32, name=f"h_codes{first}", align_bytes=64)
             h_bytes = sb.tile([P, count], U8, name=f"h_bytes{first}", align_bytes=64)
             nc.vector.quantize_mx(
-                out=h_codes[:].bitcast(FP8X4), scales=h_bytes[:], in_=h_bf[first][:].rearrange("p j t -> p (j t)")
+                out=h_codes[:].bitcast(FP8X4), scales=h_bytes[:], in_=h_bf[first].rearrange("p j t -> p (j t)")
             )
             if first == 0:
                 res = [ps.tile([P, count], F32, name=f"res{first}_{b}")[:] for b in range(2)]
@@ -198,4 +199,5 @@ def tile_picked_posadd_gelu_p_kernel(tc, x_words, x_scales, w1, w2, pe, offs, ou
             else:
                 staged = sb.tile([P, 2, count], F32, name=f"staged{first}")
                 nc.vector.tensor_copy(staged[:], both[:])
-                nc.sync.dma_start(out_rows[:, :, cols], staged[:])
+                for b in range(2):
+                    nc.sync.dma_start(out_rows[:, b, cols], staged[:, b, :])

@@ -18,8 +18,7 @@ ADD = mybir.AluOpType.add
 P = 128
 PACK = 4
 PASSES = K // (P * PACK)
-HALF = S // 2
-VECTOR_M = [80, 80]
+VECTOR_M = 84
 CHUNKS = [(0, 256), (256, 128), (384, 128)]
 
 
@@ -45,7 +44,7 @@ def tile_picked_posadd_gelu_p_kernel(tc, x_words, x_scales, w1, w2, pe, offs, ou
         word_table = [sb.tile([P, T], I32, name=f"word_table{z}", align_bytes=64) for z in range(PASSES)]
         w1_raw = [sb.tile([P, PACK, H], F32, name=f"w1_raw{z}", align_bytes=64) for z in range(PASSES)]
         pe_table = [sb.tile([P, T], F32, name=f"pe_table{t}", align_bytes=64) for t in range(PACK)]
-        w2_raw = sb.tile([P, PACK, N], F32, name="w2_raw", tag="w2_then_h", align_bytes=64)
+        w2_raw = sb.tile([P, PACK, N], F32, name="w2_raw", align_bytes=64)
 
         def load_words(z):
             nc.sync.dma_start(word_table[z][:], x_words[z].rearrange("p c r -> p (c r)").bitcast(I32))
@@ -54,23 +53,22 @@ def tile_picked_posadd_gelu_p_kernel(tc, x_words, x_scales, w1, w2, pe, offs, ou
             nc.sync.dma_start(w1_raw[z][:], w1[z * 512 : (z + 1) * 512, :].rearrange("(p j) c -> p j c", j=PACK))
 
         load_words(0)
-        load_words(1)
         for q in range(4):
             nc.sync.dma_start(
                 scale_table[32 * q : 32 * q + 8, :].bitcast(I32),
                 x_scales[:, 4 * q : 4 * q + 4, :].bitcast(I32),
             )
         load_w1(0)
+        load_words(1)
         load_w1(1)
         pe_rows = pe.rearrange("(p t) c -> t p c", t=PACK)
         for t in range(PACK):
             nc.sync.dma_start(pe_table[t][:], pe_rows[t])
-            if t == 1:
-                nc.sync.dma_start(w2_raw[:], w2.rearrange("(p j) m -> p j m", j=PACK))
+        nc.sync.dma_start(w2_raw[:], w2.rearrange("(p j) m -> p j m", j=PACK))
 
         x_codes = [sb.tile([P, S], U32, name=f"x_codes{z}", align_bytes=64) for z in range(PASSES)]
         x_bytes = sb.tile([P, S], U8, name="x_bytes", align_bytes=64)
-        w1_bf = [sb.tile([P, PACK, P, PACK], BF16, name=f"w1_bf{z}", align_bytes=64) for z in range(PASSES)]
+        w1_bf = [sb.tile([P, PACK, P, PACK], BF16, name=f"w1_bf{z}", tag=f"slot{z}", align_bytes=64) for z in range(PASSES)]
         w1_codes = [sb.tile([P, H], U32, name=f"w1_codes{z}", align_bytes=64) for z in range(PASSES)]
         w1_bytes = [sb.tile([P, H], U8, name=f"w1_bytes{z}", align_bytes=64) for z in range(PASSES)]
 
@@ -80,101 +78,86 @@ def tile_picked_posadd_gelu_p_kernel(tc, x_words, x_scales, w1, w2, pe, offs, ou
         def quantize_w1(z):
             src = w1_raw[z][:].rearrange("p j (m t) -> p m t j", t=PACK)
             dst = w1_bf[z][:].rearrange("p t m j -> p m t j")
-            nc.vector.tensor_copy(dst[:, : VECTOR_M[z]], src[:, : VECTOR_M[z]])
-            nc.scalar.copy(dst[:, VECTOR_M[z] :], src[:, VECTOR_M[z] :])
+            nc.vector.tensor_copy(dst[:, :VECTOR_M], src[:, :VECTOR_M])
+            nc.scalar.copy(dst[:, VECTOR_M:], src[:, VECTOR_M:])
             nc.vector.quantize_mx(
                 out=w1_codes[z][:].bitcast(FP8X4),
                 scales=w1_bytes[z][:],
                 in_=w1_bf[z][:].rearrange("p t m j -> p (t m j)"),
             )
 
+        acc = [ps.tile([P, S], F32, name=f"acc{t}") for t in range(PACK)]
+
+        def first_product(z):
+            for t in range(PACK):
+                nc.tensor.matmul_mx(
+                    out=acc[t][:],
+                    lhsT=w1_codes[z][:, t * P : (t + 1) * P].bitcast(FP8X4),
+                    lhsT_scale=w1_bytes[z][:, t * P : (t + 1) * P],
+                    rhs=x_codes[z][:].bitcast(FP8X4),
+                    rhs_scale=x_bytes[4 * z : P, :],
+                    start=(z == 0),
+                    stop=(z == PASSES - 1),
+                )
+
         gather_words(0)
-        gather_words(1)
         nc.vector.tensor_copy(x_bytes[:], scale_table[:].indirect(offsets[:]))
         quantize_w1(0)
+        first_product(0)
+        gather_words(1)
         quantize_w1(1)
+        first_product(1)
 
-        acc = {}
-        for pair in range(2):
-            for half in range(2):
-                acc[pair, half] = ps.tile([P, 2, HALF], F32, name=f"acc{pair}{half}")
-                cols = slice(half * HALF, (half + 1) * HALF)
-                for e in range(2):
-                    t = 2 * pair + e
-                    for z in range(PASSES):
-                        nc.tensor.matmul_mx(
-                            out=acc[pair, half][:, e, :],
-                            lhsT=w1_codes[z][:, t * P : (t + 1) * P].bitcast(FP8X4),
-                            lhsT_scale=w1_bytes[z][:, t * P : (t + 1) * P],
-                            rhs=x_codes[z][:, cols].bitcast(FP8X4),
-                            rhs_scale=x_bytes[4 * z : P, cols],
-                            start=(z == 0),
-                            stop=(z == PASSES - 1),
-                        )
+        pe_picked = sb.tile([P, S], F32, name="pe_picked", tag="slot1", align_bytes=64)
+        nc.vector.tensor_copy(pe_picked[:], pe_table[0][:].indirect(offsets[:]))
+        product = {}
+        for t in range(1, PACK):
+            product[t] = sb.tile([P, S], F32, name=f"product{t}", align_bytes=64)
+            nc.scalar.copy(product[t][:], acc[t][:])
 
-        early = sb.tile([P, 2, S], F32, name="early", align_bytes=64)
-        late = sb.tile([P, 2 * S], F32, name="late", align_bytes=64)
+        pre = [sb.tile([P, 2, S], F32, name=f"pre{pair}", align_bytes=64) for pair in range(2)]
+        h_all = sb.tile([P, S, PACK], BF16, name="h_all", align_bytes=64)
 
-        def picked(pair, first, count):
-            if pair == 0:
-                return early[:, :, first : first + count]
-            if first < HALF:
-                return late[:].rearrange("p (e j) -> p e j", e=2)[:, :, first : first + count]
-            return late[:, HALF : 3 * HALF].rearrange("p (e j) -> p e j", e=2)[:, :, first - HALF : first - HALF + count]
-
-        h_all = sb.tile([P, S, PACK], BF16, name="h_all", tag="w2_then_h", align_bytes=64)
-        h_bf = {first: h_all[:, first : first + count, :] for first, count in CHUNKS}
-
-        def gather_pe(t, first, count):
-            dst = late[:, 0:S] if t == 2 else picked(t // 2, first, count)[:, t % 2, :]
-            nc.vector.tensor_copy(dst, pe_table[t][:].indirect(picks(first, count)))
-
-        def add_and_gelu(pair, first, count):
-            half, inner = divmod(first, HALF)
-            pre = sb.tile([P, 2, count], F32, name=f"pre{pair}_{first}", align_bytes=64)
+        def gather_add(t, first, count):
+            cols = slice(first, first + count)
             nc.vector.tensor_tensor(
-                pre[:], acc[pair, half][:, :, inner : inner + count], picked(pair, first, count), ADD
+                pre[t // 2][:, t % 2, cols], pe_table[t][:].indirect(picks(first, count)), product[t][:, cols], ADD
             )
-            gelu(pair, pre, first, count)
 
-        def gelu(pair, pre, first, count):
-            for start, width in CHUNKS:
-                lo, hi = max(first, start), min(first + count, start + width)
-                if lo < hi:
-                    nc.scalar.activation(
-                        h_bf[start][:, lo - start : hi - start, 2 * pair : 2 * pair + 2],
-                        pre[:, :, lo - first : hi - first].rearrange("p e j -> p j e"),
-                        GELU,
-                        bias=zero_bias[:],
-                    )
+        def gelu(pair, first, count):
+            cols = slice(first, first + count)
+            nc.scalar.activation(
+                h_all[:, cols, 2 * pair : 2 * pair + 2],
+                pre[pair][:, :, cols].rearrange("p e j -> p j e"),
+                GELU,
+                bias=zero_bias[:],
+            )
 
-        gather_pe(0, 0, S)
-        gather_pe(1, 0, S)
-        w2_bf = sb.tile([P, N, PACK], BF16, name="w2_bf", align_bytes=64)
-        nc.scalar.copy(w2_bf[:], w2_raw[:].rearrange("p j m -> p m j"))
-        add_and_gelu(0, 0, HALF)
-        add_and_gelu(0, HALF, HALF)
-        gather_pe(2, 0, S)
+        nc.vector.tensor_tensor(pre[0][:, 0, :], acc[0][:], pe_picked[:], ADD)
+        gather_add(1, 0, S)
+        gelu(0, 0, S)
+        gather_add(2, 0, S)
+        for first, count in CHUNKS:
+            gather_add(3, first, count)
+            gelu(1, first, count)
 
+        w2_bf = sb.tile([P, N, PACK], BF16, name="w2_bf", tag="w2_then_h", align_bytes=64)
+        nc.vector.tensor_copy(w2_bf[:], w2_raw[:].rearrange("p j m -> p m j"))
         w2_codes = sb.tile([P, N], U32, name="w2_codes", align_bytes=64)
         w2_bytes = sb.tile([P, N], U8, name="w2_bytes", align_bytes=64)
-        out_rows = out.rearrange("(b p) s -> p b s", p=P)
         nc.vector.quantize_mx(
             out=w2_codes[:].bitcast(FP8X4), scales=w2_bytes[:], in_=w2_bf[:].rearrange("p m j -> p (m j)")
         )
 
-        for half in range(2):
-            for quarter in range(2):
-                gather_pe(3, half * HALF + quarter * 128, 128)
-            for quarter in range(2):
-                add_and_gelu(1, half * HALF + quarter * 128, 128)
-
+        out_rows = out.rearrange("(b p) s -> p b s", p=P)
+        h_codes = sb.tile([P, S], U32, name="h_codes", tag="w2_then_h", align_bytes=64)
+        h_bytes = sb.tile([P, S], U8, name="h_bytes", align_bytes=64)
         for first, count in CHUNKS:
             cols = slice(first, first + count)
-            h_codes = sb.tile([P, count], U32, name=f"h_codes{first}", align_bytes=64)
-            h_bytes = sb.tile([P, count], U8, name=f"h_bytes{first}", align_bytes=64)
             nc.vector.quantize_mx(
-                out=h_codes[:].bitcast(FP8X4), scales=h_bytes[:], in_=h_bf[first].rearrange("p j t -> p (j t)")
+                out=h_codes[:, cols].bitcast(FP8X4),
+                scales=h_bytes[:, cols],
+                in_=h_all[:, cols, :].rearrange("p j t -> p (j t)"),
             )
             if first == 0:
                 res = [ps.tile([P, count], F32, name=f"res{first}_{b}")[:] for b in range(2)]
@@ -186,8 +169,8 @@ def tile_picked_posadd_gelu_p_kernel(tc, x_words, x_scales, w1, w2, pe, offs, ou
                     out=res[b],
                     lhsT=w2_codes[:, b * P : (b + 1) * P].bitcast(FP8X4),
                     lhsT_scale=w2_bytes[:, b * P : (b + 1) * P],
-                    rhs=h_codes[:].bitcast(FP8X4),
-                    rhs_scale=h_bytes[:],
+                    rhs=h_codes[:, cols].bitcast(FP8X4),
+                    rhs_scale=h_bytes[:, cols],
                     start=True,
                     stop=True,
                 )

@@ -19,7 +19,8 @@ P = 128
 PACK = 4
 PASSES = K // (P * PACK)
 VECTOR_M = 84
-CHUNKS = [(0, 256), (256, 128), (384, 128)]
+QUARTER = 128
+CHUNKS = [(first, QUARTER) for first in range(0, S, QUARTER)]
 
 
 def tile_picked_posadd_gelu_p_kernel(tc, x_words, x_scales, w1, w2, pe, offs, out):
@@ -61,14 +62,14 @@ def tile_picked_posadd_gelu_p_kernel(tc, x_words, x_scales, w1, w2, pe, offs, ou
         load_w1(0)
         load_words(1)
         load_w1(1)
+        nc.sync.dma_start(w2_raw[:], w2.rearrange("(p j) m -> p j m", j=PACK))
         pe_rows = pe.rearrange("(p t) c -> t p c", t=PACK)
         for t in range(PACK):
             nc.sync.dma_start(pe_table[t][:], pe_rows[t])
-        nc.sync.dma_start(w2_raw[:], w2.rearrange("(p j) m -> p j m", j=PACK))
 
         x_codes = [sb.tile([P, S], U32, name=f"x_codes{z}", align_bytes=64) for z in range(PASSES)]
         x_bytes = sb.tile([P, S], U8, name="x_bytes", align_bytes=64)
-        w1_bf = [sb.tile([P, PACK, P, PACK], BF16, name=f"w1_bf{z}", tag=f"slot{z}", align_bytes=64) for z in range(PASSES)]
+        w1_bf = [sb.tile([P, PACK, P, PACK], BF16, name=f"w1_bf{z}", align_bytes=64) for z in range(PASSES)]
         w1_codes = [sb.tile([P, H], U32, name=f"w1_codes{z}", align_bytes=64) for z in range(PASSES)]
         w1_bytes = [sb.tile([P, H], U8, name=f"w1_bytes{z}", align_bytes=64) for z in range(PASSES)]
 
@@ -108,8 +109,16 @@ def tile_picked_posadd_gelu_p_kernel(tc, x_words, x_scales, w1, w2, pe, offs, ou
         quantize_w1(1)
         first_product(1)
 
-        pe_picked = sb.tile([P, S], F32, name="pe_picked", tag="slot1", align_bytes=64)
+        pe_picked = sb.tile([P, S], F32, name="pe_picked", align_bytes=64)
         nc.vector.tensor_copy(pe_picked[:], pe_table[0][:].indirect(offsets[:]))
+        w2_bf = sb.tile([P, N, PACK], BF16, name="w2_bf", align_bytes=64)
+        nc.scalar.copy(w2_bf[:], w2_raw[:].rearrange("p j m -> p m j"))
+        w2_codes = sb.tile([P, N], U32, name="w2_codes", align_bytes=64)
+        w2_bytes = sb.tile([P, N], U8, name="w2_bytes", align_bytes=64)
+        nc.vector.quantize_mx(
+            out=w2_codes[:].bitcast(FP8X4), scales=w2_bytes[:], in_=w2_bf[:].rearrange("p m j -> p (m j)")
+        )
+
         product = {}
         for t in range(1, PACK):
             product[t] = sb.tile([P, S], F32, name=f"product{t}", align_bytes=64)
@@ -141,16 +150,8 @@ def tile_picked_posadd_gelu_p_kernel(tc, x_words, x_scales, w1, w2, pe, offs, ou
             gather_add(3, first, count)
             gelu(1, first, count)
 
-        w2_bf = sb.tile([P, N, PACK], BF16, name="w2_bf", tag="w2_then_h", align_bytes=64)
-        nc.vector.tensor_copy(w2_bf[:], w2_raw[:].rearrange("p j m -> p m j"))
-        w2_codes = sb.tile([P, N], U32, name="w2_codes", align_bytes=64)
-        w2_bytes = sb.tile([P, N], U8, name="w2_bytes", align_bytes=64)
-        nc.vector.quantize_mx(
-            out=w2_codes[:].bitcast(FP8X4), scales=w2_bytes[:], in_=w2_bf[:].rearrange("p m j -> p (m j)")
-        )
-
         out_rows = out.rearrange("(b p) s -> p b s", p=P)
-        h_codes = sb.tile([P, S], U32, name="h_codes", tag="w2_then_h", align_bytes=64)
+        h_codes = sb.tile([P, S], U32, name="h_codes", align_bytes=64)
         h_bytes = sb.tile([P, S], U8, name="h_bytes", align_bytes=64)
         for first, count in CHUNKS:
             cols = slice(first, first + count)
@@ -159,14 +160,10 @@ def tile_picked_posadd_gelu_p_kernel(tc, x_words, x_scales, w1, w2, pe, offs, ou
                 scales=h_bytes[:, cols],
                 in_=h_all[:, cols, :].rearrange("p j t -> p (j t)"),
             )
-            if first == 0:
-                res = [ps.tile([P, count], F32, name=f"res{first}_{b}")[:] for b in range(2)]
-            else:
-                both = ps.tile([P, 2, count], F32, name=f"res{first}")
-                res = [both[:, b, :] for b in range(2)]
+            res = ps.tile([P, 2, count], F32, name=f"res{first}")
             for b in range(N // P):
                 nc.tensor.matmul_mx(
-                    out=res[b],
+                    out=res[:, b, :],
                     lhsT=w2_codes[:, b * P : (b + 1) * P].bitcast(FP8X4),
                     lhsT_scale=w2_bytes[:, b * P : (b + 1) * P],
                     rhs=h_codes[:, cols].bitcast(FP8X4),
@@ -174,13 +171,9 @@ def tile_picked_posadd_gelu_p_kernel(tc, x_words, x_scales, w1, w2, pe, offs, ou
                     start=True,
                     stop=True,
                 )
-            if first == 0:
-                for b in range(2):
-                    staged = sb.tile([P, count], F32, name=f"staged{first}_{b}")
-                    nc.scalar.copy(staged[:], res[b])
-                    nc.sync.dma_start(out_rows[:, b, cols], staged[:])
+            staged = sb.tile([P, 2, count], F32, name=f"staged{first}")
+            if (first // QUARTER) % 2 == 0:
+                nc.scalar.copy(staged[:], res[:])
             else:
-                staged = sb.tile([P, 2, count], F32, name=f"staged{first}")
-                nc.vector.tensor_copy(staged[:], both[:])
-                for b in range(2):
-                    nc.sync.dma_start(out_rows[:, b, cols], staged[:, b, :])
+                nc.vector.tensor_copy(staged[:], res[:])
+            nc.sync.dma_start(out_rows[:, :, cols], staged[:])

@@ -18,7 +18,10 @@ ADD = mybir.AluOpType.add
 P = 128
 PACK = 4
 PASSES = K // (P * PACK)
-VECTOR_M = 84
+VECTOR_M = 64
+VECTOR_M_HALVES = [56, 92]
+PLAIN = 1
+FUSED = [0, 2, 3]
 QUARTER = 128
 CHUNKS = [(first, QUARTER) for first in range(0, S, QUARTER)]
 
@@ -43,15 +46,16 @@ def tile_picked_posadd_gelu_p_kernel(tc, x_words, x_scales, w1, w2, pe, offs, ou
         nc.scalar.activation(zero_bias[:], zero[:], GELU)
 
         word_table = [sb.tile([P, T], I32, name=f"word_table{z}", align_bytes=64) for z in range(PASSES)]
-        w1_raw = [sb.tile([P, PACK, H], F32, name=f"w1_raw{z}", align_bytes=64) for z in range(PASSES)]
+        w1_raw = sb.tile([P, PACK, H], F32, name="w1_raw", align_bytes=64)
+        w1_halves = [sb.tile([P, 2, H], F32, name=f"w1_half{u}", align_bytes=64) for u in range(2)]
         pe_table = [sb.tile([P, T], F32, name=f"pe_table{t}", align_bytes=64) for t in range(PACK)]
-        w2_raw = sb.tile([P, PACK, N], F32, name="w2_raw", align_bytes=64)
+        w2_raw = [sb.tile([P, 2, N], F32, name=f"w2_raw{u}", tag=("w2_first", "w2_then_h")[u], align_bytes=64) for u in range(2)]
+        w2_rows = w2.rearrange("(p j) m -> p j m", j=PACK)
 
         def load_words(z):
             nc.sync.dma_start(word_table[z][:], x_words[z].rearrange("p c r -> p (c r)").bitcast(I32))
 
-        def load_w1(z):
-            nc.sync.dma_start(w1_raw[z][:], w1[z * 512 : (z + 1) * 512, :].rearrange("(p j) c -> p j c", j=PACK))
+        w1_rows = w1.rearrange("(z p j) c -> z p j c", z=PASSES, j=PACK)
 
         load_words(0)
         for q in range(4):
@@ -59,13 +63,16 @@ def tile_picked_posadd_gelu_p_kernel(tc, x_words, x_scales, w1, w2, pe, offs, ou
                 scale_table[32 * q : 32 * q + 8, :].bitcast(I32),
                 x_scales[:, 4 * q : 4 * q + 4, :].bitcast(I32),
             )
-        load_w1(0)
+        nc.sync.dma_start(w1_raw[:], w1_rows[0])
         load_words(1)
-        load_w1(1)
-        nc.sync.dma_start(w2_raw[:], w2.rearrange("(p j) m -> p j m", j=PACK))
+        for u in range(2):
+            nc.sync.dma_start(w1_halves[u][:], w1_rows[1][:, 2 * u : 2 * u + 2, :])
+        nc.sync.dma_start(w2_raw[0][:], w2_rows[:, 0:2, :])
         pe_rows = pe.rearrange("(p t) c -> t p c", t=PACK)
-        for t in range(PACK):
+        for t in [PLAIN] + FUSED:
             nc.sync.dma_start(pe_table[t][:], pe_rows[t])
+            if t == FUSED[0]:
+                nc.sync.dma_start(w2_raw[1][:], w2_rows[:, 2:4, :])
 
         x_codes = [sb.tile([P, S], U32, name=f"x_codes{z}", align_bytes=64) for z in range(PASSES)]
         x_bytes = sb.tile([P, S], U8, name="x_bytes", align_bytes=64)
@@ -76,21 +83,24 @@ def tile_picked_posadd_gelu_p_kernel(tc, x_words, x_scales, w1, w2, pe, offs, ou
         def gather_words(z):
             nc.vector.tensor_copy(x_codes[z][:], word_table[z][:].bitcast(U32).indirect(offsets[:]))
 
-        def quantize_w1(z):
-            src = w1_raw[z][:].rearrange("p j (m t) -> p m t j", t=PACK)
-            dst = w1_bf[z][:].rearrange("p t m j -> p m t j")
-            nc.vector.tensor_copy(dst[:, :VECTOR_M], src[:, :VECTOR_M])
-            nc.scalar.copy(dst[:, VECTOR_M:], src[:, VECTOR_M:])
+        def cast_w1(z, raw, rows, vector_m):
+            src = raw[:].rearrange("p j (m t) -> p m t j", t=PACK)
+            dst = w1_bf[z][:].rearrange("p t m j -> p m t j")[:, :, :, rows]
+            nc.vector.tensor_copy(dst[:, :vector_m], src[:, :vector_m])
+            nc.scalar.copy(dst[:, vector_m:], src[:, vector_m:])
+
+        def quantize_w1(z, first, count):
+            cols = slice(first * P, (first + count) * P)
             nc.vector.quantize_mx(
-                out=w1_codes[z][:].bitcast(FP8X4),
-                scales=w1_bytes[z][:],
-                in_=w1_bf[z][:].rearrange("p t m j -> p (t m j)"),
+                out=w1_codes[z][:, cols].bitcast(FP8X4),
+                scales=w1_bytes[z][:, cols],
+                in_=w1_bf[z][:, first : first + count].rearrange("p t m j -> p (t m j)"),
             )
 
         acc = [ps.tile([P, S], F32, name=f"acc{t}") for t in range(PACK)]
 
         def first_product(z):
-            for t in range(PACK):
+            for t in FUSED + [PLAIN]:
                 nc.tensor.matmul_mx(
                     out=acc[t][:],
                     lhsT=w1_codes[z][:, t * P : (t + 1) * P].bitcast(FP8X4),
@@ -103,29 +113,34 @@ def tile_picked_posadd_gelu_p_kernel(tc, x_words, x_scales, w1, w2, pe, offs, ou
 
         gather_words(0)
         nc.vector.tensor_copy(x_bytes[:], scale_table[:].indirect(offsets[:]))
-        quantize_w1(0)
+        cast_w1(0, w1_raw, slice(0, PACK), VECTOR_M)
+        quantize_w1(0, 0, PACK)
         first_product(0)
         gather_words(1)
-        quantize_w1(1)
+        for u in range(2):
+            cast_w1(1, w1_halves[u], slice(2 * u, 2 * u + 2), VECTOR_M_HALVES[u])
+        quantize_w1(1, 0, 2)
+        quantize_w1(1, 2, 2)
         first_product(1)
 
         pe_picked = sb.tile([P, S], F32, name="pe_picked", align_bytes=64)
-        nc.vector.tensor_copy(pe_picked[:], pe_table[0][:].indirect(offsets[:]))
+        nc.vector.tensor_copy(pe_picked[:], pe_table[PLAIN][:].indirect(offsets[:]))
+        product = {}
+        for t in FUSED:
+            product[t] = sb.tile([P, S], F32, name=f"product{t}", align_bytes=64)
+            nc.scalar.copy(product[t][:], acc[t][:])
+
         w2_bf = sb.tile([P, N, PACK], BF16, name="w2_bf", align_bytes=64)
-        nc.scalar.copy(w2_bf[:], w2_raw[:].rearrange("p j m -> p m j"))
+        for u in range(2):
+            nc.scalar.copy(w2_bf[:, :, 2 * u : 2 * u + 2], w2_raw[u][:].rearrange("p j m -> p m j"))
         w2_codes = sb.tile([P, N], U32, name="w2_codes", align_bytes=64)
         w2_bytes = sb.tile([P, N], U8, name="w2_bytes", align_bytes=64)
         nc.vector.quantize_mx(
             out=w2_codes[:].bitcast(FP8X4), scales=w2_bytes[:], in_=w2_bf[:].rearrange("p m j -> p (m j)")
         )
 
-        product = {}
-        for t in range(1, PACK):
-            product[t] = sb.tile([P, S], F32, name=f"product{t}", align_bytes=64)
-            nc.scalar.copy(product[t][:], acc[t][:])
-
         pre = [sb.tile([P, 2, S], F32, name=f"pre{pair}", align_bytes=64) for pair in range(2)]
-        h_all = sb.tile([P, S, PACK], BF16, name="h_all", align_bytes=64)
+        h_all = sb.tile([P, S, PACK], BF16, name="h_all", tag="w2_then_h", align_bytes=64)
 
         def gather_add(t, first, count):
             cols = slice(first, first + count)
@@ -142,8 +157,8 @@ def tile_picked_posadd_gelu_p_kernel(tc, x_words, x_scales, w1, w2, pe, offs, ou
                 bias=zero_bias[:],
             )
 
-        nc.vector.tensor_tensor(pre[0][:, 0, :], acc[0][:], pe_picked[:], ADD)
-        gather_add(1, 0, S)
+        gather_add(0, 0, S)
+        nc.vector.tensor_tensor(pre[0][:, PLAIN, :], acc[PLAIN][:], pe_picked[:], ADD)
         gelu(0, 0, S)
         gather_add(2, 0, S)
         for first, count in CHUNKS:

@@ -33,7 +33,6 @@ def tile_picked_posadd_gelu_p_kernel(tc, x_words, x_scales, w1, w2, pe, offs, ou
         ps = ctx.enter_context(tc.psum_pool(name="ps", bufs=1))
 
         offsets = sb.tile([P, S // 16], U16, name="offsets")
-        nc.sync.dma_start(offsets[:], offs)
 
         def picks(first, count):
             return offsets[:, first // 16 : (first + count) // 16]
@@ -58,6 +57,7 @@ def tile_picked_posadd_gelu_p_kernel(tc, x_words, x_scales, w1, w2, pe, offs, ou
         w1_rows = w1.rearrange("(z p j) c -> z p j c", z=PASSES, j=PACK)
 
         load_words(0)
+        nc.sync.dma_start(offsets[:], offs)
         for q in range(4):
             nc.sync.dma_start(
                 scale_table[32 * q : 32 * q + 8, :].bitcast(I32),
@@ -97,7 +97,7 @@ def tile_picked_posadd_gelu_p_kernel(tc, x_words, x_scales, w1, w2, pe, offs, ou
                 in_=w1_bf[z][:, first : first + count].rearrange("p t m j -> p (t m j)"),
             )
 
-        acc = [ps.tile([P, S], F32, name=f"acc{t}") for t in range(PACK)]
+        acc = [ps.tile([P, S], F32, name=f"acc{t}", tag=f"bank{t}") for t in range(PACK)]
 
         def first_product(z):
             for t in FUSED + [PLAIN]:
@@ -175,10 +175,14 @@ def tile_picked_posadd_gelu_p_kernel(tc, x_words, x_scales, w1, w2, pe, offs, ou
                 scales=h_bytes[:, cols],
                 in_=h_all[:, cols, :].rearrange("p j t -> p (j t)"),
             )
-            res = ps.tile([P, 2, count], F32, name=f"res{first}")
+            if first + count < S:
+                both = ps.tile([P, 2, count], F32, name=f"res{first}")
+                res = [both[:, b, :] for b in range(2)]
+            else:
+                res = [ps.tile([P, count], F32, name=f"res{first}_{b}", tag=f"bank{2 * b}")[:] for b in range(2)]
             for b in range(N // P):
                 nc.tensor.matmul_mx(
-                    out=res[:, b, :],
+                    out=res[b],
                     lhsT=w2_codes[:, b * P : (b + 1) * P].bitcast(FP8X4),
                     lhsT_scale=w2_bytes[:, b * P : (b + 1) * P],
                     rhs=h_codes[:, cols].bitcast(FP8X4),
@@ -186,9 +190,16 @@ def tile_picked_posadd_gelu_p_kernel(tc, x_words, x_scales, w1, w2, pe, offs, ou
                     start=True,
                     stop=True,
                 )
-            staged = sb.tile([P, 2, count], F32, name=f"staged{first}")
-            if (first // QUARTER) % 2 == 0:
-                nc.scalar.copy(staged[:], res[:])
+            if first + count < S:
+                staged = sb.tile([P, 2, count], F32, name=f"staged{first}")
+                if (first // QUARTER) % 2 == 0:
+                    nc.scalar.copy(staged[:], both[:])
+                else:
+                    nc.vector.tensor_copy(staged[:], both[:])
+                nc.sync.dma_start(out_rows[:, :, cols], staged[:])
             else:
-                nc.vector.tensor_copy(staged[:], res[:])
-            nc.sync.dma_start(out_rows[:, :, cols], staged[:])
+                staged = [sb.tile([P, count], F32, name=f"staged{first}_{b}") for b in range(2)]
+                nc.vector.tensor_copy(staged[0][:], res[0])
+                nc.sync.dma_start(out_rows[:, 0, cols], staged[0][:])
+                nc.scalar.copy(staged[1][:], res[1])
+                nc.scalar.dma_start(out_rows[:, 1, cols], staged[1][:])

@@ -18,7 +18,7 @@ ADD = mybir.AluOpType.add
 P = 128
 PACK = 4
 PASSES = K // (P * PACK)
-VECTOR_M = 64
+VECTOR_M = 84
 VECTOR_M_HALVES = [56, 92]
 PLAIN = 1
 FUSED = [0, 2, 3]

@@ -126,26 +126,26 @@ def tile_picked_posadd_gelu_p_kernel(tc, x_words, x_scales, w1, w2, pe, offs, ou
         pe_picked = sb.tile([P, S], F32, name="pe_picked", align_bytes=64)
         nc.vector.tensor_copy(pe_picked[:], pe_table[PLAIN][:].indirect(offsets[:]))
         product = {}
-        for t in FUSED:
-            product[t] = sb.tile([P, S], F32, name=f"product{t}", align_bytes=64)
-            nc.scalar.copy(product[t][:], acc[t][:])
+        for t, first, count in [(0, 0, S), (2, 0, S), (3, 0, QUARTER), (3, QUARTER, S - QUARTER)]:
+            tag = "product_then_w2" if count == QUARTER else f"product{t}"
+            piece = sb.tile([P, count], F32, name=f"product{t}_{first}", tag=tag, align_bytes=64)
+            nc.scalar.copy(piece[:], acc[t][:, first : first + count])
+            product[t, first] = piece
 
         w2_bf = sb.tile([P, N, PACK], BF16, name="w2_bf", align_bytes=64)
         for u in range(2):
             nc.scalar.copy(w2_bf[:, :, 2 * u : 2 * u + 2], w2_raw[u][:].rearrange("p j m -> p m j"))
-        w2_codes = sb.tile([P, N], U32, name="w2_codes", align_bytes=64)
-        w2_bytes = sb.tile([P, N], U8, name="w2_bytes", align_bytes=64)
-        nc.vector.quantize_mx(
-            out=w2_codes[:].bitcast(FP8X4), scales=w2_bytes[:], in_=w2_bf[:].rearrange("p m j -> p (m j)")
-        )
-
         pre = [sb.tile([P, 2, S], F32, name=f"pre{pair}", align_bytes=64) for pair in range(2)]
         h_all = sb.tile([P, S, PACK], BF16, name="h_all", tag="w2_then_h", align_bytes=64)
 
         def gather_add(t, first, count):
             cols = slice(first, first + count)
+            start = min(first, QUARTER)
             nc.vector.tensor_tensor(
-                pre[t // 2][:, t % 2, cols], pe_table[t][:].indirect(picks(first, count)), product[t][:, cols], ADD
+                pre[t // 2][:, t % 2, cols],
+                pe_table[t][:].indirect(picks(first, count)),
+                product[t, start][:, first - start : first - start + count],
+                ADD,
             )
 
         def gelu(pair, first, count):
@@ -161,7 +161,16 @@ def tile_picked_posadd_gelu_p_kernel(tc, x_words, x_scales, w1, w2, pe, offs, ou
         nc.vector.tensor_tensor(pre[0][:, PLAIN, :], acc[PLAIN][:], pe_picked[:], ADD)
         gelu(0, 0, S)
         gather_add(2, 0, S)
-        for first, count in CHUNKS:
+        for first, count in CHUNKS[:2]:
+            gather_add(3, first, count)
+            gelu(1, first, count)
+        w2_codes = sb.tile([P, N], U32, name="w2_codes", tag="product_then_w2", align_bytes=64)
+        w2_bytes = sb.tile([P, N], U8, name="w2_bytes", align_bytes=64)
+        nc.vector.quantize_mx(
+            out=w2_codes[:].bitcast(FP8X4), scales=w2_bytes[:], in_=w2_bf[:].rearrange("p m j -> p (m j)")
+        )
+
+        for first, count in CHUNKS[2:]:
             gather_add(3, first, count)
             gelu(1, first, count)
 

@@ -22,6 +22,7 @@ VECTOR_M = 84
 VECTOR_M_HALVES = [56, 92]
 PLAIN = 1
 FUSED = [0, 2, 3]
+HALF = S // 2
 QUARTER = 128
 CHUNKS = [(first, QUARTER) for first in range(0, S, QUARTER)]
 
@@ -126,16 +127,25 @@ def tile_picked_posadd_gelu_p_kernel(tc, x_words, x_scales, w1, w2, pe, offs, ou
         pe_picked = sb.tile([P, S], F32, name="pe_picked", align_bytes=64)
         nc.vector.tensor_copy(pe_picked[:], pe_table[PLAIN][:].indirect(offsets[:]))
         product = {}
-        for t, first, count in [(0, 0, S), (2, 0, S), (3, 0, QUARTER), (3, QUARTER, S - QUARTER)]:
-            tag = "product_then_w2" if count == QUARTER else f"product{t}"
-            piece = sb.tile([P, count], F32, name=f"product{t}_{first}", tag=tag, align_bytes=64)
-            nc.scalar.copy(piece[:], acc[t][:, first : first + count])
-            product[t, first] = piece
 
+        def copy_product(t, first, count):
+            tag = "product_then_w2" if count == QUARTER else f"product{t}"
+            product[t, first] = sb.tile([P, count], F32, name=f"product{t}_{first}", tag=tag, align_bytes=64)
+            nc.scalar.copy(product[t, first][:], acc[t][:, first : first + count])
+
+        first_pair = sb.tile([P, 2 * S + HALF], F32, name="first_pair", align_bytes=64)
+        halves = [first_pair[:, S : S + HALF], first_pair[:, 2 * S : 2 * S + HALF]]
+        for u in range(2):
+            nc.scalar.copy(halves[u], acc[0][:, u * HALF : (u + 1) * HALF])
+        copy_product(2, 0, S)
         w2_bf = sb.tile([P, N, PACK], BF16, name="w2_bf", align_bytes=64)
         for u in range(2):
             nc.scalar.copy(w2_bf[:, :, 2 * u : 2 * u + 2], w2_raw[u][:].rearrange("p j m -> p m j"))
-        pre = [sb.tile([P, 2, S], F32, name=f"pre{pair}", align_bytes=64) for pair in range(2)]
+        copy_product(3, 0, QUARTER)
+        copy_product(3, QUARTER, S - QUARTER)
+
+        second_pair = sb.tile([P, 2 * S], F32, name="second_pair", align_bytes=64)
+        pre = [pair[:, : 2 * S].rearrange("p (e j) -> p e j", e=2) for pair in (first_pair, second_pair)]
         h_all = sb.tile([P, S, PACK], BF16, name="h_all", tag="w2_then_h", align_bytes=64)
 
         def gather_add(t, first, count):
@@ -157,7 +167,13 @@ def tile_picked_posadd_gelu_p_kernel(tc, x_words, x_scales, w1, w2, pe, offs, ou
                 bias=zero_bias[:],
             )
 
-        gather_add(0, 0, S)
+        for u in range(2):
+            nc.vector.tensor_tensor(
+                pre[0][:, 0, u * HALF : (u + 1) * HALF],
+                pe_table[0][:].indirect(picks(u * HALF, HALF)),
+                halves[u],
+                ADD,
+            )
         nc.vector.tensor_tensor(pre[0][:, PLAIN, :], acc[PLAIN][:], pe_picked[:], ADD)
         gelu(0, 0, S)
         gather_add(2, 0, S)

@@ -19,7 +19,7 @@ P = 128
 PACK = 4
 PASSES = K // (P * PACK)
 VECTOR_M = 84
-VECTOR_M_HALVES = [56, 92]
+VECTOR_M_HALVES = [44, 84]
 PLAIN = 1
 FUSED = [0, 2, 3]
 HALF = S // 2
@@ -98,16 +98,18 @@ def tile_picked_posadd_gelu_p_kernel(tc, x_words, x_scales, w1, w2, pe, offs, ou
                 in_=w1_bf[z][:, first : first + count].rearrange("p t m j -> p (t m j)"),
             )
 
-        acc = [ps.tile([P, S], F32, name=f"acc{t}", tag=f"bank{t}") for t in range(PACK)]
+        groups = [(0, 0, HALF), (0, HALF, HALF)] + [(t, 0, S) for t in FUSED[1:] + [PLAIN]]
+        acc = {(t, first): ps.tile([P, count], F32, name=f"acc{t}_{first}", tag=f"bank{g}") for g, (t, first, count) in enumerate(groups)}
 
         def first_product(z):
-            for t in FUSED + [PLAIN]:
+            for t, first, count in groups:
+                cols = slice(first, first + count)
                 nc.tensor.matmul_mx(
-                    out=acc[t][:],
+                    out=acc[t, first][:],
                     lhsT=w1_codes[z][:, t * P : (t + 1) * P].bitcast(FP8X4),
                     lhsT_scale=w1_bytes[z][:, t * P : (t + 1) * P],
-                    rhs=x_codes[z][:].bitcast(FP8X4),
-                    rhs_scale=x_bytes[4 * z : P, :],
+                    rhs=x_codes[z][:, cols].bitcast(FP8X4),
+                    rhs_scale=x_bytes[4 * z : P, cols],
                     start=(z == 0),
                     stop=(z == PASSES - 1),
                 )
@@ -129,20 +131,21 @@ def tile_picked_posadd_gelu_p_kernel(tc, x_words, x_scales, w1, w2, pe, offs, ou
         product = {}
 
         def copy_product(t, first, count):
-            tag = "product_then_w2" if count == QUARTER else f"product{t}"
+            tag = "product_then_w2" if (t, first) == (3, HALF) else f"product{t}_{first}"
             product[t, first] = sb.tile([P, count], F32, name=f"product{t}_{first}", tag=tag, align_bytes=64)
-            nc.scalar.copy(product[t, first][:], acc[t][:, first : first + count])
+            nc.scalar.copy(product[t, first][:], acc[t, 0][:, first : first + count])
 
-        first_pair = sb.tile([P, 2 * S + HALF], F32, name="first_pair", align_bytes=64)
-        halves = [first_pair[:, S : S + HALF], first_pair[:, 2 * S : 2 * S + HALF]]
+        first_pair = sb.tile([P, 2 * S], F32, name="first_pair", align_bytes=64)
+        halves = [first_pair[:, S + u * HALF : S + (u + 1) * HALF] for u in range(2)]
         for u in range(2):
-            nc.scalar.copy(halves[u], acc[0][:, u * HALF : (u + 1) * HALF])
+            nc.scalar.copy(halves[u], acc[0, u * HALF][:])
         copy_product(2, 0, S)
         w2_bf = sb.tile([P, N, PACK], BF16, name="w2_bf", align_bytes=64)
         for u in range(2):
             nc.scalar.copy(w2_bf[:, :, 2 * u : 2 * u + 2], w2_raw[u][:].rearrange("p j m -> p m j"))
-        copy_product(3, 0, QUARTER)
-        copy_product(3, QUARTER, S - QUARTER)
+        copy_product(3, 0, HALF)
+        copy_product(3, HALF, QUARTER)
+        copy_product(3, HALF + QUARTER, QUARTER)
 
         second_pair = sb.tile([P, 2 * S], F32, name="second_pair", align_bytes=64)
         pre = [pair[:, : 2 * S].rearrange("p (e j) -> p e j", e=2) for pair in (first_pair, second_pair)]
@@ -150,7 +153,7 @@ def tile_picked_posadd_gelu_p_kernel(tc, x_words, x_scales, w1, w2, pe, offs, ou
 
         def gather_add(t, first, count):
             cols = slice(first, first + count)
-            start = min(first, QUARTER)
+            start = first if first >= HALF else 0
             nc.vector.tensor_tensor(
                 pre[t // 2][:, t % 2, cols],
                 pe_table[t][:].indirect(picks(first, count)),
@@ -174,21 +177,23 @@ def tile_picked_posadd_gelu_p_kernel(tc, x_words, x_scales, w1, w2, pe, offs, ou
                 halves[u],
                 ADD,
             )
-        nc.vector.tensor_tensor(pre[0][:, PLAIN, :], acc[PLAIN][:], pe_picked[:], ADD)
-        gelu(0, 0, S)
+        for u in range(2):
+            cols = slice(u * HALF, (u + 1) * HALF)
+            nc.vector.tensor_tensor(pre[0][:, PLAIN, cols], acc[PLAIN, 0][:, cols], pe_picked[:, cols], ADD)
+            gelu(0, u * HALF, HALF)
         gather_add(2, 0, S)
         for first, count in CHUNKS[:2]:
             gather_add(3, first, count)
             gelu(1, first, count)
+        for first, count in CHUNKS[2:]:
+            gather_add(3, first, count)
+            gelu(1, first, count)
+
         w2_codes = sb.tile([P, N], U32, name="w2_codes", tag="product_then_w2", align_bytes=64)
         w2_bytes = sb.tile([P, N], U8, name="w2_bytes", align_bytes=64)
         nc.vector.quantize_mx(
             out=w2_codes[:].bitcast(FP8X4), scales=w2_bytes[:], in_=w2_bf[:].rearrange("p m j -> p (m j)")
         )
-
-        for first, count in CHUNKS[2:]:
-            gather_add(3, first, count)
-            gelu(1, first, count)
 
         out_rows = out.rearrange("(b p) s -> p b s", p=P)
         h_codes = sb.tile([P, S], U32, name="h_codes", align_bytes=64)

@@ -18,13 +18,16 @@ ADD = mybir.AluOpType.add
 P = 128
 PACK = 4
 PASSES = K // (P * PACK)
-VECTOR_M = 84
-VECTOR_M_HALVES = [44, 84]
+HALF = S // 2
+QUARTER = S // 4
+QUARTERS = [(first, QUARTER) for first in range(0, S, QUARTER)]
+
+VECTOR_PASS0 = 78
+VECTOR_FIRST_ROWS = 32
+VECTOR_LAST_ROWS = 48
+W2_ROWS = [slice(0, 1), slice(1, PACK)]
 PLAIN = 1
 FUSED = [0, 2, 3]
-HALF = S // 2
-QUARTER = 128
-CHUNKS = [(first, QUARTER) for first in range(0, S, QUARTER)]
 
 
 def tile_picked_posadd_gelu_p_kernel(tc, x_words, x_scales, w1, w2, pe, offs, out):
@@ -49,7 +52,10 @@ def tile_picked_posadd_gelu_p_kernel(tc, x_words, x_scales, w1, w2, pe, offs, ou
         w1_raw = sb.tile([P, PACK, H], F32, name="w1_raw", align_bytes=64)
         w1_halves = [sb.tile([P, 2, H], F32, name=f"w1_half{u}", align_bytes=64) for u in range(2)]
         pe_table = [sb.tile([P, T], F32, name=f"pe_table{t}", align_bytes=64) for t in range(PACK)]
-        w2_raw = [sb.tile([P, 2, N], F32, name=f"w2_raw{u}", tag=("w2_first", "w2_then_h")[u], align_bytes=64) for u in range(2)]
+        w2_raw = [
+            sb.tile([P, rows.stop - rows.start, N], F32, name=f"w2_raw{u}", tag=("w2_first", "w2_then_h")[u], align_bytes=64)
+            for u, rows in enumerate(W2_ROWS)
+        ]
         w2_rows = w2.rearrange("(p j) m -> p j m", j=PACK)
 
         def load_words(z):
@@ -68,12 +74,12 @@ def tile_picked_posadd_gelu_p_kernel(tc, x_words, x_scales, w1, w2, pe, offs, ou
         load_words(1)
         for u in range(2):
             nc.sync.dma_start(w1_halves[u][:], w1_rows[1][:, 2 * u : 2 * u + 2, :])
-        nc.sync.dma_start(w2_raw[0][:], w2_rows[:, 0:2, :])
+        nc.sync.dma_start(w2_raw[0][:], w2_rows[:, W2_ROWS[0], :])
         pe_rows = pe.rearrange("(p t) c -> t p c", t=PACK)
         for t in [PLAIN] + FUSED:
             nc.sync.dma_start(pe_table[t][:], pe_rows[t])
             if t == FUSED[0]:
-                nc.sync.dma_start(w2_raw[1][:], w2_rows[:, 2:4, :])
+                nc.sync.dma_start(w2_raw[1][:], w2_rows[:, W2_ROWS[1], :])
 
         x_codes = [sb.tile([P, S], U32, name=f"x_codes{z}", align_bytes=64) for z in range(PASSES)]
         x_bytes = sb.tile([P, S], U8, name="x_bytes", align_bytes=64)
@@ -84,11 +90,15 @@ def tile_picked_posadd_gelu_p_kernel(tc, x_words, x_scales, w1, w2, pe, offs, ou
         def gather_words(z):
             nc.vector.tensor_copy(x_codes[z][:], word_table[z][:].bitcast(U32).indirect(offsets[:]))
 
-        def cast_w1(z, raw, rows, vector_m):
-            src = raw[:].rearrange("p j (m t) -> p m t j", t=PACK)
-            dst = w1_bf[z][:].rearrange("p t m j -> p m t j")[:, :, :, rows]
-            nc.vector.tensor_copy(dst[:, :vector_m], src[:, :vector_m])
-            nc.scalar.copy(dst[:, vector_m:], src[:, vector_m:])
+        def cast_views(z, raw, rows, planes):
+            dst = w1_bf[z][:].rearrange("p t m j -> p m t j")[:, :, planes, rows]
+            src = raw[:].rearrange("p j (m t) -> p m t j", t=PACK)[:, :, planes, :]
+            return dst, src
+
+        def cast_shared(z, raw, rows, planes, vector_columns):
+            dst, src = cast_views(z, raw, rows, planes)
+            nc.vector.tensor_copy(dst[:, :vector_columns], src[:, :vector_columns])
+            nc.scalar.copy(dst[:, vector_columns:], src[:, vector_columns:])
 
         def quantize_w1(z, first, count):
             cols = slice(first * P, (first + count) * P)
@@ -99,7 +109,10 @@ def tile_picked_posadd_gelu_p_kernel(tc, x_words, x_scales, w1, w2, pe, offs, ou
             )
 
         groups = [(0, 0, HALF), (0, HALF, HALF)] + [(t, 0, S) for t in FUSED[1:] + [PLAIN]]
-        acc = {(t, first): ps.tile([P, count], F32, name=f"acc{t}_{first}", tag=f"bank{g}") for g, (t, first, count) in enumerate(groups)}
+        acc = {
+            (t, first): ps.tile([P, count], F32, name=f"acc{t}_{first}", tag=f"bank{g}")
+            for g, (t, first, count) in enumerate(groups)
+        }
 
         def first_product(z):
             for t, first, count in groups:
@@ -114,14 +127,16 @@ def tile_picked_posadd_gelu_p_kernel(tc, x_words, x_scales, w1, w2, pe, offs, ou
                     stop=(z == PASSES - 1),
                 )
 
+        all_four, low, high = slice(0, PACK), slice(0, 2), slice(2, PACK)
         gather_words(0)
         nc.vector.tensor_copy(x_bytes[:], scale_table[:].indirect(offsets[:]))
-        cast_w1(0, w1_raw, slice(0, PACK), VECTOR_M)
+        cast_shared(0, w1_raw, all_four, all_four, VECTOR_PASS0)
         quantize_w1(0, 0, PACK)
         first_product(0)
         gather_words(1)
-        for u in range(2):
-            cast_w1(1, w1_halves[u], slice(2 * u, 2 * u + 2), VECTOR_M_HALVES[u])
+        cast_shared(1, w1_halves[0], low, all_four, VECTOR_FIRST_ROWS)
+        nc.vector.tensor_copy(*cast_views(1, w1_halves[1], high, low))
+        cast_shared(1, w1_halves[1], high, high, VECTOR_LAST_ROWS)
         quantize_w1(1, 0, 2)
         quantize_w1(1, 2, 2)
         first_product(1)
@@ -136,19 +151,19 @@ def tile_picked_posadd_gelu_p_kernel(tc, x_words, x_scales, w1, w2, pe, offs, ou
             nc.scalar.copy(product[t, first][:], acc[t, 0][:, first : first + count])
 
         first_pair = sb.tile([P, 2 * S], F32, name="first_pair", align_bytes=64)
-        halves = [first_pair[:, S + u * HALF : S + (u + 1) * HALF] for u in range(2)]
+        parked = [first_pair[:, S + u * HALF : S + (u + 1) * HALF] for u in range(2)]
         for u in range(2):
-            nc.scalar.copy(halves[u], acc[0, u * HALF][:])
+            nc.scalar.copy(parked[u], acc[0, u * HALF][:])
         copy_product(2, 0, S)
         w2_bf = sb.tile([P, N, PACK], BF16, name="w2_bf", align_bytes=64)
-        for u in range(2):
-            nc.scalar.copy(w2_bf[:, :, 2 * u : 2 * u + 2], w2_raw[u][:].rearrange("p j m -> p m j"))
+        for raw, rows in zip(w2_raw, W2_ROWS):
+            nc.scalar.copy(w2_bf[:, :, rows], raw[:].rearrange("p j m -> p m j"))
         copy_product(3, 0, HALF)
         copy_product(3, HALF, QUARTER)
         copy_product(3, HALF + QUARTER, QUARTER)
 
         second_pair = sb.tile([P, 2 * S], F32, name="second_pair", align_bytes=64)
-        pre = [pair[:, : 2 * S].rearrange("p (e j) -> p e j", e=2) for pair in (first_pair, second_pair)]
+        pre = [pair[:].rearrange("p (e s) -> p e s", e=2) for pair in (first_pair, second_pair)]
         h_all = sb.tile([P, S, PACK], BF16, name="h_all", tag="w2_then_h", align_bytes=64)
 
         def gather_add(t, first, count):
@@ -165,7 +180,7 @@ def tile_picked_posadd_gelu_p_kernel(tc, x_words, x_scales, w1, w2, pe, offs, ou
             cols = slice(first, first + count)
             nc.scalar.activation(
                 h_all[:, cols, 2 * pair : 2 * pair + 2],
-                pre[pair][:, :, cols].rearrange("p e j -> p j e"),
+                pre[pair][:, :, cols].rearrange("p e s -> p s e"),
                 GELU,
                 bias=zero_bias[:],
             )
@@ -174,7 +189,7 @@ def tile_picked_posadd_gelu_p_kernel(tc, x_words, x_scales, w1, w2, pe, offs, ou
             nc.vector.tensor_tensor(
                 pre[0][:, 0, u * HALF : (u + 1) * HALF],
                 pe_table[0][:].indirect(picks(u * HALF, HALF)),
-                halves[u],
+                parked[u],
                 ADD,
             )
         for u in range(2):
@@ -182,10 +197,7 @@ def tile_picked_posadd_gelu_p_kernel(tc, x_words, x_scales, w1, w2, pe, offs, ou
             nc.vector.tensor_tensor(pre[0][:, PLAIN, cols], acc[PLAIN, 0][:, cols], pe_picked[:, cols], ADD)
             gelu(0, u * HALF, HALF)
         gather_add(2, 0, S)
-        for first, count in CHUNKS[:2]:
-            gather_add(3, first, count)
-            gelu(1, first, count)
-        for first, count in CHUNKS[2:]:
+        for first, count in QUARTERS:
             gather_add(3, first, count)
             gelu(1, first, count)
 
@@ -198,18 +210,19 @@ def tile_picked_posadd_gelu_p_kernel(tc, x_words, x_scales, w1, w2, pe, offs, ou
         out_rows = out.rearrange("(b p) s -> p b s", p=P)
         h_codes = sb.tile([P, S], U32, name="h_codes", align_bytes=64)
         h_bytes = sb.tile([P, S], U8, name="h_bytes", align_bytes=64)
-        for first, count in CHUNKS:
+        for c, (first, count) in enumerate(QUARTERS):
             cols = slice(first, first + count)
+            is_last = c == len(QUARTERS) - 1
             nc.vector.quantize_mx(
                 out=h_codes[:, cols].bitcast(FP8X4),
                 scales=h_bytes[:, cols],
-                in_=h_all[:, cols, :].rearrange("p j t -> p (j t)"),
+                in_=h_all[:, cols, :].rearrange("p s t -> p (s t)"),
             )
-            if first + count < S:
+            if is_last:
+                res = [ps.tile([P, count], F32, name=f"res{first}_{b}", tag=f"bank{2 * b}")[:] for b in range(2)]
+            else:
                 both = ps.tile([P, 2, count], F32, name=f"res{first}")
                 res = [both[:, b, :] for b in range(2)]
-            else:
-                res = [ps.tile([P, count], F32, name=f"res{first}_{b}", tag=f"bank{2 * b}")[:] for b in range(2)]
             for b in range(N // P):
                 nc.tensor.matmul_mx(
                     out=res[b],
@@ -220,16 +233,16 @@ def tile_picked_posadd_gelu_p_kernel(tc, x_words, x_scales, w1, w2, pe, offs, ou
                     start=True,
                     stop=True,
                 )
-            if first + count < S:
+            if is_last:
+                blocks = [sb.tile([P, count], F32, name=f"staged{first}_{b}") for b in range(2)]
+                nc.vector.tensor_copy(blocks[0][:], res[0])
+                nc.sync.dma_start(out_rows[:, 0, cols], blocks[0][:])
+                nc.scalar.copy(blocks[1][:], res[1])
+                nc.scalar.dma_start(out_rows[:, 1, cols], blocks[1][:])
+            else:
                 staged = sb.tile([P, 2, count], F32, name=f"staged{first}")
-                if (first // QUARTER) % 2 == 0:
+                if c % 2 == 0:
                     nc.scalar.copy(staged[:], both[:])
                 else:
                     nc.vector.tensor_copy(staged[:], both[:])
                 nc.sync.dma_start(out_rows[:, :, cols], staged[:])
-            else:
-                staged = [sb.tile([P, count], F32, name=f"staged{first}_{b}") for b in range(2)]
-                nc.vector.tensor_copy(staged[0][:], res[0])
-                nc.sync.dma_start(out_rows[:, 0, cols], staged[0][:])
-                nc.scalar.copy(staged[1][:], res[1])
-                nc.scalar.dma_start(out_rows[:, 1, cols], staged[1][:])

@@ -131,7 +131,8 @@ def tile_picked_posadd_gelu_p_kernel(tc, x_words, x_scales, w1, w2, pe, offs, ou
         gather_words(0)
         nc.vector.tensor_copy(x_bytes[:], scale_table[:].indirect(offsets[:]))
         cast_shared(0, w1_raw, all_four, all_four, VECTOR_PASS0)
-        quantize_w1(0, 0, PACK)
+        quantize_w1(0, 0, 1)
+        quantize_w1(0, 1, PACK - 1)
         first_product(0)
         gather_words(1)
         cast_shared(1, w1_halves[0], low, all_four, VECTOR_FIRST_ROWS)

@@ -22,7 +22,7 @@ HALF = S // 2
 QUARTER = S // 4
 QUARTERS = [(first, QUARTER) for first in range(0, S, QUARTER)]
 
-VECTOR_PASS0 = 78
+VECTOR_PASS0 = 92
 VECTOR_FIRST_ROWS = 32
 VECTOR_LAST_ROWS = 48
 W2_ROWS = [slice(0, 1), slice(1, PACK)]

@@ -22,7 +22,7 @@ HALF = S // 2
 QUARTER = S // 4
 QUARTERS = [(first, QUARTER) for first in range(0, S, QUARTER)]
 
-VECTOR_PASS0 = 92
+VECTOR_PASS0 = 80
 VECTOR_FIRST_ROWS = 32
 VECTOR_LAST_ROWS = 48
 W2_ROWS = [slice(0, 1), slice(1, PACK)]
@@ -65,13 +65,13 @@ def tile_picked_posadd_gelu_p_kernel(tc, x_words, x_scales, w1, w2, pe, offs, ou
 
         load_words(0)
         nc.sync.dma_start(offsets[:], offs)
+        load_words(1)
         for q in range(4):
             nc.sync.dma_start(
                 scale_table[32 * q : 32 * q + 8, :].bitcast(I32),
                 x_scales[:, 4 * q : 4 * q + 4, :].bitcast(I32),
             )
         nc.sync.dma_start(w1_raw[:], w1_rows[0])
-        load_words(1)
         for u in range(2):
             nc.sync.dma_start(w1_halves[u][:], w1_rows[1][:, 2 * u : 2 * u + 2, :])
         nc.sync.dma_start(w2_raw[0][:], w2_rows[:, W2_ROWS[0], :])
@@ -129,13 +129,13 @@ def tile_picked_posadd_gelu_p_kernel(tc, x_words, x_scales, w1, w2, pe, offs, ou
 
         all_four, low, high = slice(0, PACK), slice(0, 2), slice(2, PACK)
         gather_words(0)
+        gather_words(1)
         nc.vector.tensor_copy(x_bytes[:], scale_table[:].indirect(offsets[:]))
         cast_shared(0, w1_raw, all_four, all_four, VECTOR_PASS0)
+        cast_shared(1, w1_halves[0], low, all_four, VECTOR_FIRST_ROWS)
         quantize_w1(0, 0, 1)
         quantize_w1(0, 1, PACK - 1)
         first_product(0)
-        gather_words(1)
-        cast_shared(1, w1_halves[0], low, all_four, VECTOR_FIRST_ROWS)
         nc.vector.tensor_copy(*cast_views(1, w1_halves[1], high, low))
         cast_shared(1, w1_halves[1], high, high, VECTOR_LAST_ROWS)
         quantize_w1(1, 0, 2)

@@ -108,13 +108,13 @@ def tile_picked_posadd_gelu_p_kernel(tc, x_words, x_scales, w1, w2, pe, offs, ou
                 in_=w1_bf[z][:, first : first + count].rearrange("p t m j -> p (t m j)"),
             )
 
-        groups = [(0, 0, HALF), (0, HALF, HALF)] + [(t, 0, S) for t in FUSED[1:] + [PLAIN]]
+        copied = [(0, 0, HALF), (0, HALF, HALF)] + [(t, 0, S) for t in FUSED[1:]]
         acc = {
             (t, first): ps.tile([P, count], F32, name=f"acc{t}_{first}", tag=f"bank{g}")
-            for g, (t, first, count) in enumerate(groups)
+            for g, (t, first, count) in enumerate(copied)
         }
 
-        def first_product(z):
+        def first_product(z, groups):
             for t, first, count in groups:
                 cols = slice(first, first + count)
                 nc.tensor.matmul_mx(
@@ -135,12 +135,12 @@ def tile_picked_posadd_gelu_p_kernel(tc, x_words, x_scales, w1, w2, pe, offs, ou
         cast_shared(1, w1_halves[0], low, all_four, VECTOR_FIRST_ROWS)
         quantize_w1(0, 0, 1)
         quantize_w1(0, 1, PACK - 1)
-        first_product(0)
+        first_product(0, copied)
         nc.vector.tensor_copy(*cast_views(1, w1_halves[1], high, low))
         cast_shared(1, w1_halves[1], high, high, VECTOR_LAST_ROWS)
         quantize_w1(1, 0, 2)
         quantize_w1(1, 2, 2)
-        first_product(1)
+        first_product(1, copied)
 
         pe_picked = sb.tile([P, S], F32, name="pe_picked", align_bytes=64)
         nc.vector.tensor_copy(pe_picked[:], pe_table[PLAIN][:].indirect(offsets[:]))
@@ -155,6 +155,9 @@ def tile_picked_posadd_gelu_p_kernel(tc, x_words, x_scales, w1, w2, pe, offs, ou
         parked = [first_pair[:, S + u * HALF : S + (u + 1) * HALF] for u in range(2)]
         for u in range(2):
             nc.scalar.copy(parked[u], acc[0, u * HALF][:])
+        acc[PLAIN, 0] = ps.tile([P, S], F32, name="acc_plain", tag="bank0")
+        for z in range(PASSES):
+            first_product(z, [(PLAIN, 0, S)])
         copy_product(2, 0, S)
         w2_bf = sb.tile([P, N, PACK], BF16, name="w2_bf", align_bytes=64)
         for raw, rows in zip(w2_raw, W2_ROWS):

@@ -138,8 +138,8 @@ def tile_picked_posadd_gelu_p_kernel(tc, x_words, x_scales, w1, w2, pe, offs, ou
         first_product(0, copied)
         nc.vector.tensor_copy(*cast_views(1, w1_halves[1], high, low))
         cast_shared(1, w1_halves[1], high, high, VECTOR_LAST_ROWS)
-        quantize_w1(1, 0, 2)
-        quantize_w1(1, 2, 2)
+        quantize_w1(1, 0, 1)
+        quantize_w1(1, 1, PACK - 1)
         first_product(1, copied)
 
         pe_picked = sb.tile([P, S], F32, name="pe_picked", align_bytes=64)

@@ -16,6 +16,7 @@ GELU = mybir.ActivationFunctionType.Gelu_apprx_tanh
 ADD = mybir.AluOpType.add
 
 P = 128
+ALIGN = 256
 PACK = 4
 PASSES = K // (P * PACK)
 HALF = S // 2
@@ -41,19 +42,19 @@ def tile_picked_posadd_gelu_p_kernel(tc, x_words, x_scales, w1, w2, pe, offs, ou
         def picks(first, count):
             return offsets[:, first // 16 : (first + count) // 16]
 
-        scale_table = sb.tile([P, T], U8, name="scale_table", align_bytes=64)
+        scale_table = sb.tile([P, T], U8, name="scale_table", align_bytes=ALIGN)
         nc.vector.memset(scale_table[:].bitcast(I32), 0)
         zero = sb.tile([P, 1], F32, name="zero")
         nc.vector.memset(zero[:], 0.0)
         zero_bias = sb.tile([P, 1], F32, name="zero_bias")
         nc.scalar.activation(zero_bias[:], zero[:], GELU)
 
-        word_table = [sb.tile([P, T], I32, name=f"word_table{z}", align_bytes=64) for z in range(PASSES)]
-        w1_raw = sb.tile([P, PACK, H], F32, name="w1_raw", align_bytes=64)
-        w1_halves = [sb.tile([P, 2, H], F32, name=f"w1_half{u}", align_bytes=64) for u in range(2)]
-        pe_table = [sb.tile([P, T], F32, name=f"pe_table{t}", align_bytes=64) for t in range(PACK)]
+        word_table = [sb.tile([P, T], I32, name=f"word_table{z}", align_bytes=ALIGN) for z in range(PASSES)]
+        w1_raw = sb.tile([P, PACK, H], F32, name="w1_raw", align_bytes=ALIGN)
+        w1_halves = [sb.tile([P, 2, H], F32, name=f"w1_half{u}", align_bytes=ALIGN) for u in range(2)]
+        pe_table = [sb.tile([P, T], F32, name=f"pe_table{t}", align_bytes=ALIGN) for t in range(PACK)]
         w2_raw = [
-            sb.tile([P, rows.stop - rows.start, N], F32, name=f"w2_raw{u}", tag=("w2_first", "w2_then_h")[u], align_bytes=64)
+            sb.tile([P, rows.stop - rows.start, N], F32, name=f"w2_raw{u}", tag=("w2_first", "w2_then_h")[u], align_bytes=ALIGN)
             for u, rows in enumerate(W2_ROWS)
         ]
         w2_rows = w2.rearrange("(p j) m -> p j m", j=PACK)
@@ -81,11 +82,11 @@ def tile_picked_posadd_gelu_p_kernel(tc, x_words, x_scales, w1, w2, pe, offs, ou
             if t == FUSED[0]:
                 nc.sync.dma_start(w2_raw[1][:], w2_rows[:, W2_ROWS[1], :])
 
-        x_codes = [sb.tile([P, S], U32, name=f"x_codes{z}", align_bytes=64) for z in range(PASSES)]
-        x_bytes = sb.tile([P, S], U8, name="x_bytes", align_bytes=64)
-        w1_bf = [sb.tile([P, PACK, P, PACK], BF16, name=f"w1_bf{z}", align_bytes=64) for z in range(PASSES)]
-        w1_codes = [sb.tile([P, H], U32, name=f"w1_codes{z}", align_bytes=64) for z in range(PASSES)]
-        w1_bytes = [sb.tile([P, H], U8, name=f"w1_bytes{z}", align_bytes=64) for z in range(PASSES)]
+        x_codes = [sb.tile([P, S], U32, name=f"x_codes{z}", align_bytes=ALIGN) for z in range(PASSES)]
+        x_bytes = sb.tile([P, S], U8, name="x_bytes", align_bytes=ALIGN)
+        w1_bf = [sb.tile([P, PACK, P, PACK], BF16, name=f"w1_bf{z}", align_bytes=ALIGN) for z in range(PASSES)]
+        w1_codes = [sb.tile([P, H], U32, name=f"w1_codes{z}", align_bytes=ALIGN) for z in range(PASSES)]
+        w1_bytes = [sb.tile([P, H], U8, name=f"w1_bytes{z}", align_bytes=ALIGN) for z in range(PASSES)]
 
         def gather_words(z):
             nc.vector.tensor_copy(x_codes[z][:], word_table[z][:].bitcast(U32).indirect(offsets[:]))
@@ -142,16 +143,16 @@ def tile_picked_posadd_gelu_p_kernel(tc, x_words, x_scales, w1, w2, pe, offs, ou
         quantize_w1(1, 1, PACK - 1)
         first_product(1, copied)
 
-        pe_picked = sb.tile([P, S], F32, name="pe_picked", align_bytes=64)
+        pe_picked = sb.tile([P, S], F32, name="pe_picked", align_bytes=ALIGN)
         nc.vector.tensor_copy(pe_picked[:], pe_table[PLAIN][:].indirect(offsets[:]))
         product = {}
 
         def copy_product(t, first, count):
             tag = "product_then_w2" if (t, first) == (3, HALF) else f"product{t}_{first}"
-            product[t, first] = sb.tile([P, count], F32, name=f"product{t}_{first}", tag=tag, align_bytes=64)
+            product[t, first] = sb.tile([P, count], F32, name=f"product{t}_{first}", tag=tag, align_bytes=ALIGN)
             nc.scalar.copy(product[t, first][:], acc[t, 0][:, first : first + count])
 
-        first_pair = sb.tile([P, 2 * S], F32, name="first_pair", align_bytes=64)
+        first_pair = sb.tile([P, 2 * S], F32, name="first_pair", align_bytes=ALIGN)
         parked = [first_pair[:, S + u * HALF : S + (u + 1) * HALF] for u in range(2)]
         for u in range(2):
             nc.scalar.copy(parked[u], acc[0, u * HALF][:])
@@ -159,16 +160,16 @@ def tile_picked_posadd_gelu_p_kernel(tc, x_words, x_scales, w1, w2, pe, offs, ou
         for z in range(PASSES):
             first_product(z, [(PLAIN, 0, S)])
         copy_product(2, 0, S)
-        w2_bf = sb.tile([P, N, PACK], BF16, name="w2_bf", align_bytes=64)
+        w2_bf = sb.tile([P, N, PACK], BF16, name="w2_bf", align_bytes=ALIGN)
         for raw, rows in zip(w2_raw, W2_ROWS):
             nc.scalar.copy(w2_bf[:, :, rows], raw[:].rearrange("p j m -> p m j"))
         copy_product(3, 0, HALF)
         copy_product(3, HALF, QUARTER)
         copy_product(3, HALF + QUARTER, QUARTER)
 
-        second_pair = sb.tile([P, 2 * S], F32, name="second_pair", align_bytes=64)
+        second_pair = sb.tile([P, 2 * S], F32, name="second_pair", align_bytes=ALIGN)
         pre = [pair[:].rearrange("p (e s) -> p e s", e=2) for pair in (first_pair, second_pair)]
-        h_all = sb.tile([P, S, PACK], BF16, name="h_all", tag="w2_then_h", align_bytes=64)
+        h_all = sb.tile([P, S, PACK], BF16, name="h_all", tag="w2_then_h", align_bytes=ALIGN)
 
         def gather_add(t, first, count):
             cols = slice(first, first + count)
@@ -205,15 +206,15 @@ def tile_picked_posadd_gelu_p_kernel(tc, x_words, x_scales, w1, w2, pe, offs, ou
             gather_add(3, first, count)
             gelu(1, first, count)
 
-        w2_codes = sb.tile([P, N], U32, name="w2_codes", tag="product_then_w2", align_bytes=64)
-        w2_bytes = sb.tile([P, N], U8, name="w2_bytes", align_bytes=64)
+        w2_codes = sb.tile([P, N], U32, name="w2_codes", tag="product_then_w2", align_bytes=ALIGN)
+        w2_bytes = sb.tile([P, N], U8, name="w2_bytes", align_bytes=ALIGN)
         nc.vector.quantize_mx(
             out=w2_codes[:].bitcast(FP8X4), scales=w2_bytes[:], in_=w2_bf[:].rearrange("p m j -> p (m j)")
         )
 
         out_rows = out.rearrange("(b p) s -> p b s", p=P)
-        h_codes = sb.tile([P, S], U32, name="h_codes", align_bytes=64)
-        h_bytes = sb.tile([P, S], U8, name="h_bytes", align_bytes=64)
+        h_codes = sb.tile([P, S], U32, name="h_codes", align_bytes=ALIGN)
+        h_bytes = sb.tile([P, S], U8, name="h_bytes", align_bytes=ALIGN)
         for c, (first, count) in enumerate(QUARTERS):
             cols = slice(first, first + count)
             is_last = c == len(QUARTERS) - 1
@@ -238,13 +239,13 @@ def tile_picked_posadd_gelu_p_kernel(tc, x_words, x_scales, w1, w2, pe, offs, ou
                     stop=True,
                 )
             if is_last:
-                blocks = [sb.tile([P, count], F32, name=f"staged{first}_{b}") for b in range(2)]
+                blocks = [sb.tile([P, count], F32, name=f"staged{first}_{b}", align_bytes=ALIGN) for b in range(2)]
                 nc.vector.tensor_copy(blocks[0][:], res[0])
                 nc.sync.dma_start(out_rows[:, 0, cols], blocks[0][:])
                 nc.scalar.copy(blocks[1][:], res[1])
                 nc.scalar.dma_start(out_rows[:, 1, cols], blocks[1][:])
             else:
-                staged = sb.tile([P, 2, count], F32, name=f"staged{first}")
+                staged = sb.tile([P, 2, count], F32, name=f"staged{first}", align_bytes=ALIGN)
                 if c % 2 == 0:
                     nc.scalar.copy(staged[:], both[:])
                 else:

from contextlib import ExitStack

import concourse.mybir as mybir

K, T, S, H, N = 1024, 1024, 512, 512, 256
FLOPS = 2 * K * H * S + 2 * H * N * S

F32 = mybir.dt.float32
BF16 = mybir.dt.bfloat16
I32 = mybir.dt.int32
U32 = mybir.dt.uint32
U16 = mybir.dt.uint16
U8 = mybir.dt.uint8
FP8X4 = mybir.dt.float8_e4m3fn_x4
GELU = mybir.ActivationFunctionType.Gelu_apprx_tanh
ADD = mybir.AluOpType.add

P = 128
ALIGN = 256
PACK = 4
PASSES = K // (P * PACK)
HALF = S // 2
QUARTER = S // 4
QUARTERS = [(first, QUARTER) for first in range(0, S, QUARTER)]

VECTOR_PASS0 = 80
VECTOR_FIRST_ROWS = 32
VECTOR_LAST_ROWS = 48
W2_ROWS = [slice(0, 1), slice(1, PACK)]
PLAIN = 1
FUSED = [0, 2, 3]


def tile_picked_posadd_gelu_p_kernel(tc, x_words, x_scales, w1, w2, pe, offs, out):
    nc = tc.nc
    with ExitStack() as ctx:
        sb = ctx.enter_context(tc.tile_pool(name="sb", bufs=1))
        ps = ctx.enter_context(tc.psum_pool(name="ps", bufs=1))

        offsets = sb.tile([P, S // 16], U16, name="offsets")

        def picks(first, count):
            return offsets[:, first // 16 : (first + count) // 16]

        scale_table = sb.tile([P, T], U8, name="scale_table", align_bytes=ALIGN)
        nc.vector.memset(scale_table[:].bitcast(I32), 0)
        zero = sb.tile([P, 1], F32, name="zero")
        nc.vector.memset(zero[:], 0.0)
        zero_bias = sb.tile([P, 1], F32, name="zero_bias")
        nc.scalar.activation(zero_bias[:], zero[:], GELU)

        word_table = [sb.tile([P, T], I32, name=f"word_table{z}", align_bytes=ALIGN) for z in range(PASSES)]
        w1_raw = sb.tile([P, PACK, H], F32, name="w1_raw", align_bytes=ALIGN)
        w1_halves = [sb.tile([P, 2, H], F32, name=f"w1_half{u}", align_bytes=ALIGN) for u in range(2)]
        pe_table = [sb.tile([P, T], F32, name=f"pe_table{t}", align_bytes=ALIGN) for t in range(PACK)]
        w2_raw = [
            sb.tile([P, rows.stop - rows.start, N], F32, name=f"w2_raw{u}", tag=("w2_first", "w2_then_h")[u], align_bytes=ALIGN)
            for u, rows in enumerate(W2_ROWS)
        ]
        w2_rows = w2.rearrange("(p j) m -> p j m", j=PACK)

        def load_words(z):
            nc.sync.dma_start(word_table[z][:], x_words[z].rearrange("p c r -> p (c r)").bitcast(I32))

        w1_rows = w1.rearrange("(z p j) c -> z p j c", z=PASSES, j=PACK)

        load_words(0)
        nc.sync.dma_start(offsets[:], offs)
        load_words(1)
        for q in range(4):
            nc.sync.dma_start(
                scale_table[32 * q : 32 * q + 8, :].bitcast(I32),
                x_scales[:, 4 * q : 4 * q + 4, :].bitcast(I32),
            )
        nc.sync.dma_start(w1_raw[:], w1_rows[0])
        for u in range(2):
            nc.sync.dma_start(w1_halves[u][:], w1_rows[1][:, 2 * u : 2 * u + 2, :])
        nc.sync.dma_start(w2_raw[0][:], w2_rows[:, W2_ROWS[0], :])
        pe_rows = pe.rearrange("(p t) c -> t p c", t=PACK)
        for t in [PLAIN] + FUSED:
            nc.sync.dma_start(pe_table[t][:], pe_rows[t])
            if t == FUSED[0]:
                nc.sync.dma_start(w2_raw[1][:], w2_rows[:, W2_ROWS[1], :])

        x_codes = [sb.tile([P, S], U32, name=f"x_codes{z}", align_bytes=ALIGN) for z in range(PASSES)]
        x_bytes = sb.tile([P, S], U8, name="x_bytes", align_bytes=ALIGN)
        w1_bf = [sb.tile([P, PACK, P, PACK], BF16, name=f"w1_bf{z}", align_bytes=ALIGN) for z in range(PASSES)]
        w1_codes = [sb.tile([P, H], U32, name=f"w1_codes{z}", align_bytes=ALIGN) for z in range(PASSES)]
        w1_bytes = [sb.tile([P, H], U8, name=f"w1_bytes{z}", align_bytes=ALIGN) for z in range(PASSES)]

        def gather_words(z):
            nc.vector.tensor_copy(x_codes[z][:], word_table[z][:].bitcast(U32).indirect(offsets[:]))

        def cast_views(z, raw, rows, planes):
            dst = w1_bf[z][:].rearrange("p t m j -> p m t j")[:, :, planes, rows]
            src = raw[:].rearrange("p j (m t) -> p m t j", t=PACK)[:, :, planes, :]
            return dst, src

        def cast_shared(z, raw, rows, planes, vector_columns):
            dst, src = cast_views(z, raw, rows, planes)
            nc.vector.tensor_copy(dst[:, :vector_columns], src[:, :vector_columns])
            nc.scalar.copy(dst[:, vector_columns:], src[:, vector_columns:])

        def quantize_w1(z, first, count):
            cols = slice(first * P, (first + count) * P)
            nc.vector.quantize_mx(
                out=w1_codes[z][:, cols].bitcast(FP8X4),
                scales=w1_bytes[z][:, cols],
                in_=w1_bf[z][:, first : first + count].rearrange("p t m j -> p (t m j)"),
            )

        copied = [(0, 0, HALF), (0, HALF, HALF)] + [(t, 0, S) for t in FUSED[1:]]
        acc = {
            (t, first): ps.tile([P, count], F32, name=f"acc{t}_{first}", tag=f"bank{g}")
            for g, (t, first, count) in enumerate(copied)
        }

        def first_product(z, groups):
            for t, first, count in groups:
                cols = slice(first, first + count)
                nc.tensor.matmul_mx(
                    out=acc[t, first][:],
                    lhsT=w1_codes[z][:, t * P : (t + 1) * P].bitcast(FP8X4),
                    lhsT_scale=w1_bytes[z][:, t * P : (t + 1) * P],
                    rhs=x_codes[z][:, cols].bitcast(FP8X4),
                    rhs_scale=x_bytes[4 * z : P, cols],
                    start=(z == 0),
                    stop=(z == PASSES - 1),
                )

        all_four, low, high = slice(0, PACK), slice(0, 2), slice(2, PACK)
        gather_words(0)
        gather_words(1)
        nc.vector.tensor_copy(x_bytes[:], scale_table[:].indirect(offsets[:]))
        cast_shared(0, w1_raw, all_four, all_four, VECTOR_PASS0)
        cast_shared(1, w1_halves[0], low, all_four, VECTOR_FIRST_ROWS)
        quantize_w1(0, 0, 1)
        quantize_w1(0, 1, PACK - 1)
        first_product(0, copied)
        nc.vector.tensor_copy(*cast_views(1, w1_halves[1], high, low))
        cast_shared(1, w1_halves[1], high, high, VECTOR_LAST_ROWS)
        quantize_w1(1, 0, 1)
        quantize_w1(1, 1, PACK - 1)
        first_product(1, copied)

        pe_picked = sb.tile([P, S], F32, name="pe_picked", align_bytes=ALIGN)
        nc.vector.tensor_copy(pe_picked[:], pe_table[PLAIN][:].indirect(offsets[:]))
        product = {}

        def copy_product(t, first, count):
            tag = "product_then_w2" if (t, first) == (3, HALF) else f"product{t}_{first}"
            product[t, first] = sb.tile([P, count], F32, name=f"product{t}_{first}", tag=tag, align_bytes=ALIGN)
            nc.scalar.copy(product[t, first][:], acc[t, 0][:, first : first + count])

        first_pair = sb.tile([P, 2 * S], F32, name="first_pair", align_bytes=ALIGN)
        parked = [first_pair[:, S + u * HALF : S + (u + 1) * HALF] for u in range(2)]
        for u in range(2):
            nc.scalar.copy(parked[u], acc[0, u * HALF][:])
        acc[PLAIN, 0] = ps.tile([P, S], F32, name="acc_plain", tag="bank0")
        for z in range(PASSES):
            first_product(z, [(PLAIN, 0, S)])
        copy_product(2, 0, S)
        w2_bf = sb.tile([P, N, PACK], BF16, name="w2_bf", align_bytes=ALIGN)
        for raw, rows in zip(w2_raw, W2_ROWS):
            nc.scalar.copy(w2_bf[:, :, rows], raw[:].rearrange("p j m -> p m j"))
        copy_product(3, 0, HALF)
        copy_product(3, HALF, QUARTER)
        copy_product(3, HALF + QUARTER, QUARTER)

        second_pair = sb.tile([P, 2 * S], F32, name="second_pair", align_bytes=ALIGN)
        pre = [pair[:].rearrange("p (e s) -> p e s", e=2) for pair in (first_pair, second_pair)]
        h_all = sb.tile([P, S, PACK], BF16, name="h_all", tag="w2_then_h", align_bytes=ALIGN)

        def gather_add(t, first, count):
            cols = slice(first, first + count)
            start = first if first >= HALF else 0
            nc.vector.tensor_tensor(
                pre[t // 2][:, t % 2, cols],
                pe_table[t][:].indirect(picks(first, count)),
                product[t, start][:, first - start : first - start + count],
                ADD,
            )

        def gelu(pair, first, count):
            cols = slice(first, first + count)
            nc.scalar.activation(
                h_all[:, cols, 2 * pair : 2 * pair + 2],
                pre[pair][:, :, cols].rearrange("p e s -> p s e"),
                GELU,
                bias=zero_bias[:],
            )

        for u in range(2):
            nc.vector.tensor_tensor(
                pre[0][:, 0, u * HALF : (u + 1) * HALF],
                pe_table[0][:].indirect(picks(u * HALF, HALF)),
                parked[u],
                ADD,
            )
        for u in range(2):
            cols = slice(u * HALF, (u + 1) * HALF)
            nc.vector.tensor_tensor(pre[0][:, PLAIN, cols], acc[PLAIN, 0][:, cols], pe_picked[:, cols], ADD)
            gelu(0, u * HALF, HALF)
        gather_add(2, 0, S)
        for first, count in QUARTERS:
            gather_add(3, first, count)
            gelu(1, first, count)

        w2_codes = sb.tile([P, N], U32, name="w2_codes", tag="product_then_w2", align_bytes=ALIGN)
        w2_bytes = sb.tile([P, N], U8, name="w2_bytes", align_bytes=ALIGN)
        nc.vector.quantize_mx(
            out=w2_codes[:].bitcast(FP8X4), scales=w2_bytes[:], in_=w2_bf[:].rearrange("p m j -> p (m j)")
        )

        out_rows = out.rearrange("(b p) s -> p b s", p=P)
        h_codes = sb.tile([P, S], U32, name="h_codes", align_bytes=ALIGN)
        h_bytes = sb.tile([P, S], U8, name="h_bytes", align_bytes=ALIGN)
        for c, (first, count) in enumerate(QUARTERS):
            cols = slice(first, first + count)
            is_last = c == len(QUARTERS) - 1
            nc.vector.quantize_mx(
                out=h_codes[:, cols].bitcast(FP8X4),
                scales=h_bytes[:, cols],
                in_=h_all[:, cols, :].rearrange("p s t -> p (s t)"),
            )
            if is_last:
                res = [ps.tile([P, count], F32, name=f"res{first}_{b}", tag=f"bank{2 * b}")[:] for b in range(2)]
            else:
                both = ps.tile([P, 2, count], F32, name=f"res{first}")
                res = [both[:, b, :] for b in range(2)]
            for b in range(N // P):
                nc.tensor.matmul_mx(
                    out=res[b],
                    lhsT=w2_codes[:, b * P : (b + 1) * P].bitcast(FP8X4),
                    lhsT_scale=w2_bytes[:, b * P : (b + 1) * P],
                    rhs=h_codes[:, cols].bitcast(FP8X4),
                    rhs_scale=h_bytes[:, cols],
                    start=True,
                    stop=True,
                )
            if is_last:
                blocks = [sb.tile([P, count], F32, name=f"staged{first}_{b}", align_bytes=ALIGN) for b in range(2)]
                nc.vector.tensor_copy(blocks[0][:], res[0])
                nc.sync.dma_start(out_rows[:, 0, cols], blocks[0][:])
                nc.scalar.copy(blocks[1][:], res[1])
                nc.scalar.dma_start(out_rows[:, 1, cols], blocks[1][:])
            else:
                staged = sb.tile([P, 2, count], F32, name=f"staged{first}", align_bytes=ALIGN)
                if c % 2 == 0:
                    nc.scalar.copy(staged[:], both[:])
                else:
                    nc.vector.tensor_copy(staged[:], both[:])
                nc.sync.dma_start(out_rows[:, :, cols], staged[:])
